import numpy as np
import ml_dtypes


def mxq(x, axis, fmt="e4m3"):
    dtype, down = {"e4m3": (ml_dtypes.float8_e4m3fn, 7), "e5m2": (ml_dtypes.float8_e5m2, 14)}[fmt]
    v = np.moveaxis(np.asarray(x, np.float32).astype(ml_dtypes.bfloat16).astype(np.float64), axis, -1)
    blocks = v.reshape(v.shape[:-1] + (-1, 32))
    amax = np.abs(blocks).max(-1, keepdims=True)
    byte = np.maximum(np.where(amax > 0, np.frexp(amax)[1] - 1 + 127, 0) - down, 1)
    scale = np.exp2(byte - 127.0)
    codes = (blocks / scale).astype(np.float32).astype(dtype).astype(np.float64)
    return np.moveaxis((codes * scale).reshape(v.shape), -1, axis)


WIDE = False


def mx_kscale(k):
    if not WIDE:
        return np.ones(k)
    levels = np.array([10, -10, 5, -5, 0])
    if k % 512:
        return np.exp2(np.random.permutation(np.resize(levels, k // 32))).repeat(32)
    a = np.empty((k // 512, 16))
    for p in range(k // 512):
        a[p, :8] = np.random.permutation(np.resize(levels, 8))
        for g in range(8):
            far = levels[np.abs(levels - a[p, g]) >= 10]
            a[p, g + 8] = far[np.random.randint(len(far))]
    return np.exp2(a.ravel()).repeat(32)


def f64(x):
    return np.asarray(x).astype(np.float64)


def striped(idx):
    return np.tile(idx.reshape(-1, 16).T, (8, 1)).astype(np.uint16)


def unstriped(offs):
    return offs[:16].T.reshape(-1).astype(np.int64)


def striped8(idx):
    return np.concatenate([x.reshape(-1, 16).T for x in idx]).astype(np.uint16)


def runs(offs, k):
    lists = np.stack([offs[16 * r : 16 * r + 16].T.reshape(-1) for r in range(8)]).astype(np.int64)
    return lists[np.arange(k) % 512 // 64]


def pack_weight(w):
    k, n = w.shape
    w = f64(np.asarray(w, np.float32).astype(ml_dtypes.bfloat16)).reshape(k // 32, 32, n)
    amax = np.abs(w).max(1)
    byte = np.clip(np.where(amax > 0, np.frexp(amax)[1] - 1 + 127 - 7, 1), 1, 254)
    scaled = (w * np.exp2(127.0 - byte)[:, None, :]).reshape(k, n).astype(np.float32)
    words = np.ascontiguousarray(scaled.reshape(k // 512, 128, 4, n).transpose(0, 1, 3, 2)).astype(ml_dtypes.float8_e4m3fn).view(np.uint8)
    return words, np.ascontiguousarray(byte.astype(np.uint8).reshape(k // 512, 16, n))


def unpack_weight(words, scales):
    g, p, n, _ = words.shape
    vals = np.ascontiguousarray(words).view(ml_dtypes.float8_e4m3fn).astype(np.float64) * np.repeat(np.exp2(scales.astype(np.float64) - 127.0), 8, axis=1)[..., None]
    return vals.transpose(0, 1, 3, 2).reshape(g * 512, n)


E2M1 = np.array([0.0, 0.5, 1.0, 1.5, 2.0, 3.0, 4.0, 6.0, -0.0, -0.5, -1.0, -1.5, -2.0, -3.0, -4.0, -6.0])


def pack_fp4(w):
    k, n = w.shape
    w = f64(np.asarray(w, np.float32).astype(ml_dtypes.bfloat16)).reshape(k // 32, 32, n)
    amax = np.abs(w).max(1)
    mant, ex = np.frexp(amax / 6.0)
    byte = np.clip(np.where(amax > 0, np.where(mant > 0.5, ex, ex - 1) + 127, 1), 1, 254)
    scaled = (w * np.exp2(127.0 - byte)[:, None, :]).reshape(k, n).astype(np.float32)
    c = np.ascontiguousarray(scaled.reshape(k // 512, 128, 4, n).transpose(0, 1, 3, 2)).astype(ml_dtypes.float4_e2m1fn).view(np.uint8) & 0xF
    words = (c[..., 0::2] | (c[..., 1::2] << 4)).reshape(k // 512, 128, 2 * n)
    return np.ascontiguousarray(words), np.ascontiguousarray(byte.astype(np.uint8).reshape(k // 512, 16, n))


def unpack_fp4(words, scales):
    g, _, n = scales.shape
    words = np.ascontiguousarray(words).reshape(g, 128, n, 2)
    nib = np.empty((g, 128, n, 4), np.uint8)
    nib[..., 0::2] = words & 0xF
    nib[..., 1::2] = words >> 4
    vals = E2M1[nib] * np.repeat(np.exp2(scales.astype(np.float64) - 127.0), 8, axis=1)[..., None]
    return vals.transpose(0, 1, 3, 2).reshape(g * 512, n)


def relu(v):
    return np.maximum(v, 0.0)

def planes(y):
    n, m = y.shape
    v = y.astype(np.float32).astype(ml_dtypes.bfloat16).astype(np.float64).reshape(n // 32, 32, m)
    top = np.abs(v).max(1)
    byte = np.clip(np.where(top > 0, np.frexp(top)[1] - 1 + 127 - 7, 1), 1, 254)
    codes = (v * np.exp2(127.0 - byte)[:, None, :]).reshape(n, m).astype(np.float32).astype(ml_dtypes.float8_e4m3fn).view(np.uint8)
    words = codes.reshape(n // 512, 128, 4, m).transpose(0, 1, 3, 2)
    return np.ascontiguousarray(words), np.ascontiguousarray(byte.astype(np.uint8).reshape(n // 512, 16, m))


K, T, S, V, N, H = 512, 2048, 512, 256, 512, 512


def setup_inputs():
    n = np.random.standard_normal
    s = mx_kscale(K)[:, None]
    u = mx_kscale(H)
    packed_xT = pack_weight(n((K, T)) * s)
    packed_w2 = pack_fp4(n((H, N)) / np.sqrt(H) / u[:, None])
    return {
        "x_words": packed_xT[0],
        "x_scales": packed_xT[1],
        "w1": (n((K, H)) / np.sqrt(K) / s * u).astype(np.float32),
        "wt": np.repeat(np.random.uniform(0.3, 1.2, (8, V)), 64, axis=0).astype(np.float32),
        "w2_words": packed_w2[0],
        "w2_scales": packed_w2[1],
        "offs": striped(np.random.permutation(T)[:S]),
        "take": striped8(np.stack([np.random.permutation(S)[:V] for _ in range(8)])),
    }


def reference(x_words, x_scales, w1, wt, w2_words, w2_scales, offs, take):
    xq = unpack_weight(x_words, x_scales)[:, unstriped(offs)]
    y = mxq(f64(w1), 0, "e4m3").T @ xq
    e = (relu(y[np.arange(H)[:, None], runs(take, H)])) * f64(wt)
    z = np.zeros((H, S))
    z[np.arange(H)[:, None], runs(take, H)] = e
    out_0 = unpack_fp4(w2_words, w2_scales).T @ mxq(z, 0, "e4m3")
    return (out_0,) + planes(out_0)

@@ -1,0 +1,191 @@
+from contextlib import ExitStack
+
+import concourse.mybir as mybir
+
+F32 = mybir.dt.float32
+BF16 = mybir.dt.bfloat16
+I32 = mybir.dt.int32
+U32 = mybir.dt.uint32
+U16 = mybir.dt.uint16
+U8 = mybir.dt.uint8
+FP8X4 = mybir.dt.float8_e4m3fn_x4
+FP4X4 = mybir.dt.float4_e2m1fn_x4
+RELU = mybir.ActivationFunctionType.Relu
+MULT = mybir.AluOpType.mult
+
+P = 128
+PACK = 4
+T, S, V, H, N = 2048, 512, 256, 512, 512
+HALF = S // 2
+CHUNK = 128
+CHUNKS = S // CHUNK
+SCALAR_M = 48
+
+FLOPS = 2 * 512 * H * S + 2 * H * N * S
+
+
+def tile_picked_echoice_relu_po_kernel(
+    tc, x_words, x_scales, w1, wt, w2_words, w2_scales, offs, take, out_0, out_1, out_2
+):
+    nc = tc.nc
+    with ExitStack() as ctx:
+        lists = ctx.enter_context(tc.tile_pool(name="lists", bufs=1))
+        sb = ctx.enter_context(tc.tile_pool(name="sb", bufs=1))
+        psum = ctx.enter_context(tc.psum_pool(name="psum", bufs=1))
+
+        offs_sb = lists.tile([P, S // 16], U16, name="offs_sb")
+        take_sb = lists.tile([P, V // 16], U16, name="take_sb")
+        nc.sync.dma_start(offs_sb[:], offs)
+        nc.sync.dma_start(take_sb[:], take)
+
+        w1_raw = sb.tile([P, PACK, H], F32, name="w1_raw", tag="w1_then_wt", align_bytes=64)
+        nc.sync.dma_start(w1_raw[:], w1.rearrange("(p j) c -> p j c", j=PACK))
+        x_tab = sb.tile([P, T], U32, name="x_tab", align_bytes=64)
+        nc.sync.dma_start(x_tab[:].bitcast(I32), x_words[0].rearrange("p n t -> p (n t)").bitcast(I32))
+
+        xs_tab = sb.tile([P, T], U8, name="xs_tab", tag="xs_then_w2", align_bytes=64)
+        nc.vector.memset(xs_tab[:].bitcast(I32), 0)
+        for q in range(4):
+            nc.scalar.dma_start(
+                xs_tab[32 * q : 32 * q + 4, :].bitcast(I32), x_scales[0, 4 * q : 4 * q + 4, :].bitcast(I32)
+            )
+        w2s_raw = sb.tile([P, N], U8, name="w2s_raw", align_bytes=64)
+        nc.gpsimd.memset(w2s_raw[:].bitcast(I32), 0)
+        for q in range(4):
+            nc.gpsimd.dma_start(
+                w2s_raw[32 * q : 32 * q + 4, :].bitcast(I32), w2_scales[0, 4 * q : 4 * q + 4, :].bitcast(I32)
+            )
+
+        z = [sb.tile([P, S], F32, name="z%d" % t) for t in range(PACK)]
+        for t in range(PACK):
+            nc.vector.memset(z[t][:], 0.0)
+        warm = sb.tile([P, 1], F32, name="warm")
+        nc.scalar.activation(warm[:], z[0][:, 0:1], RELU)
+
+        xs_pick = sb.tile([P, S], U8, name="xs_pick", align_bytes=64)
+        nc.vector.tensor_copy(xs_pick[:], xs_tab[:].indirect(offs_sb[:]))
+
+        w1_bf = sb.tile([P, PACK * H], BF16, name="w1_bf", align_bytes=64)
+        w1_dst = w1_bf[:].rearrange("p (t m j) -> p m j t", t=PACK, j=PACK)
+        w1_src = w1_raw[:].rearrange("p j (m t) -> p m j t", t=PACK)
+        nc.scalar.copy(w1_dst[:, :SCALAR_M], w1_src[:, :SCALAR_M])
+        nc.vector.tensor_copy(w1_dst[:, SCALAR_M:], w1_src[:, SCALAR_M:])
+        w1_q = sb.tile([P, H], U32, name="w1_q", align_bytes=64)
+        w1_s = sb.tile([P, H], U8, name="w1_s", align_bytes=64)
+        nc.vector.quantize_mx(out=w1_q[:].bitcast(FP8X4), scales=w1_s[:], in_=w1_bf[:])
+
+        w2_raw = sb.tile([P, 2 * N], U8, name="w2_raw", tag="xs_then_w2", align_bytes=64)
+        nc.sync.dma_start(w2_raw[:].bitcast(I32), w2_words[0].bitcast(I32))
+        wt_sb = sb.tile([P, V], F32, name="wt_sb", tag="w1_then_wt", align_bytes=64)
+        nc.sync.dma_start(wt_sb[:], wt.rearrange("(p j) v -> p j v", j=PACK)[:, 0, :])
+
+        x_pick = sb.tile([P, S], U32, name="x_pick", align_bytes=64)
+        for h in range(2):
+            nc.vector.tensor_copy(
+                x_pick[:, h * HALF : (h + 1) * HALF], x_tab[:].indirect(offs_sb[:, h * 16 : (h + 1) * 16])
+            )
+
+        w2_q = sb.tile([P, 2 * N], U8, name="w2_q", align_bytes=64)
+        w2_s = sb.tile([P, N], U8, name="w2_s", align_bytes=64)
+        nc.vector.tensor_copy(
+            w2_s[:].rearrange("p (t m) -> p m t", t=PACK), w2s_raw[:].rearrange("p (m t) -> p m t", t=PACK)
+        )
+        nc.vector.tensor_copy(
+            w2_q[:].rearrange("p (t m b) -> p m t b", t=PACK, b=2),
+            w2_raw[:].rearrange("p (m t b) -> p m t b", t=PACK, b=2),
+        )
+
+        y = [sb.tile([P, S], F32, name="y%d" % t) for t in range(PACK)]
+
+        def first_layer(t, cols, bank):
+            width = cols.stop - cols.start
+            acc = psum.tile([P, width], F32, name="acc", tag="bank%d" % bank)
+            m_cols = slice(t * P, (t + 1) * P)
+            nc.tensor.matmul_mx(
+                out=acc[:],
+                lhsT=w1_q[:, m_cols].bitcast(FP8X4),
+                lhsT_scale=w1_s[:, m_cols],
+                rhs=x_pick[:, cols].bitcast(FP8X4),
+                rhs_scale=xs_pick[:, cols],
+                start=True,
+                stop=True,
+            )
+            nc.scalar.activation(y[t][:, cols], acc[:], RELU)
+
+        first_layer(0, slice(0, HALF), 0)
+        first_layer(1, slice(0, HALF), 1)
+        first_layer(0, slice(HALF, S), 2)
+        first_layer(1, slice(HALF, S), 3)
+        first_layer(2, slice(0, S), 4)
+        first_layer(3, slice(0, S), 5)
+
+        e = [sb.tile([P, V], F32, name="e%d" % t) for t in range(PACK)]
+        z_bf = [sb.tile([P, CHUNK, PACK], BF16, name="z_bf%d" % c, align_bytes=64) for c in range(CHUNKS)]
+
+        def gather(t):
+            nc.vector.tensor_copy(e[t][:], y[t][:].indirect(take_sb[:]))
+
+        def scatter(t):
+            nc.vector.tensor_tensor(z[t][:].indirect(take_sb[:]), e[t][:], wt_sb[:], MULT)
+
+        def round_plane(t, c):
+            src = z[t][:, c * CHUNK : (c + 1) * CHUNK]
+            if t >= 2 and c == CHUNKS - 1:
+                nc.vector.tensor_copy(z_bf[c][:, :, t], src)
+            else:
+                nc.scalar.copy(z_bf[c][:, :, t], src)
+
+        gather(0)
+        for t in range(PACK):
+            if t + 1 < PACK:
+                gather(t + 1)
+            scatter(t)
+            for c in range(CHUNKS - 1):
+                round_plane(t, c)
+            if t < 2:
+                round_plane(t, CHUNKS - 1)
+        round_plane(2, CHUNKS - 1)
+        round_plane(3, CHUNKS - 1)
+
+        z_q = sb.tile([P, S], U32, name="z_q", align_bytes=64)
+        z_s = sb.tile([P, S], U8, name="z_s", align_bytes=64)
+        o_q = sb.tile([P, S], U32, name="o_q", align_bytes=64)
+        o_s = sb.tile([P, S], U8, name="o_s", align_bytes=64)
+        out_rows = out_0.rearrange("(p t) c -> p t c", t=PACK)
+        out_words = out_1[0].rearrange("p n t -> p (n t)").bitcast(I32)
+
+        accs = []
+        for c in range(CHUNKS):
+            cols = slice(c * CHUNK, (c + 1) * CHUNK)
+            nc.vector.quantize_mx(
+                out=z_q[:, cols].bitcast(FP8X4), scales=z_s[:, cols], in_=z_bf[c][:].rearrange("p n t -> p (n t)")
+            )
+            acc = psum.tile([P, PACK, CHUNK], F32, name="acc2", tag="bank%d" % ((6 + c) % 8))
+            for t in range(PACK):
+                nc.tensor.matmul_mx(
+                    out=acc[:, t, :],
+                    lhsT=w2_q[:, 2 * t * P : 2 * (t + 1) * P].bitcast(FP4X4),
+                    lhsT_scale=w2_s[:, t * P : (t + 1) * P],
+                    rhs=z_q[:, cols].bitcast(FP8X4),
+                    rhs_scale=z_s[:, cols],
+                    start=True,
+                    stop=True,
+                )
+            accs.append(acc)
+
+        for c in range(CHUNKS):
+            cols = slice(c * CHUNK, (c + 1) * CHUNK)
+            o = sb.tile([P, PACK, CHUNK], F32, name="o%d" % c)
+            nc.scalar.copy(o[:], accs[c][:])
+            nc.sync.dma_start(out_rows[:, :, cols], o[:])
+            o_bf = sb.tile([P, CHUNK * PACK], BF16, name="o_bf%d" % c, align_bytes=64)
+            nc.vector.tensor_copy(
+                o_bf[:].rearrange("p (c i t) -> p c t i", i=4, t=PACK), o[:].rearrange("p t (c i) -> p c t i", i=4)
+            )
+            nc.vector.quantize_mx(out=o_q[:, cols].bitcast(FP8X4), scales=o_s[:, cols], in_=o_bf[:])
+            if c % 2 == 1:
+                both = slice((c - 1) * CHUNK, (c + 1) * CHUNK)
+                nc.sync.dma_start(out_words[:, both], o_q[:, both].bitcast(I32))
+        for q in range(4):
+            queue = nc.sync if q % 2 == 0 else nc.scalar
+            queue.dma_start(out_2[0, 4 * q : 4 * q + 4, :].bitcast(I32), o_s[32 * q : 32 * q + 4, :].bitcast(I32))

@@ -14,14 +14,17 @@ RELU = mybir.ActivationFunctionType.Relu
 MULT = mybir.AluOpType.mult
 
 P = 128
-PACK = 4
-T, S, V, H, N = 2048, 512, 256, 512, 512
+SLOTS = 4
+GROUP = 16
+K, T, S, V, H, N = 512, 2048, 512, 256, 512, 512
 HALF = S // 2
 CHUNK = 128
 CHUNKS = S // CHUNK
-SCALAR_M = 48
+W1_SCALAR_M = 56
+VECTOR_CHUNK = 1
+LAST_SCALAR_GROUPS = 12
 
-FLOPS = 2 * 512 * H * S + 2 * H * N * S
+FLOPS = 2 * K * H * S + 2 * H * N * S
 
 
 def tile_picked_echoice_relu_po_kernel(
@@ -33,159 +36,179 @@ def tile_picked_echoice_relu_po_kernel(
         sb = ctx.enter_context(tc.tile_pool(name="sb", bufs=1))
         psum = ctx.enter_context(tc.psum_pool(name="psum", bufs=1))
 
-        offs_sb = lists.tile([P, S // 16], U16, name="offs_sb")
-        take_sb = lists.tile([P, V // 16], U16, name="take_sb")
+        def load_scale_rows_spread(rows, name):
+            spread = sb.tile([P, rows.shape[1]], U8, name=name, align_bytes=64)
+            nc.vector.memset(spread[:].bitcast(I32), 0)
+            nc.sync.dma_start(spread[0:P:8, :].bitcast(I32), rows.bitcast(I32))
+            return spread
+
+        def move_to_scale_rows(spread, name):
+            plane = sb.tile([P, spread.shape[1]], U8, name=name, align_bytes=64)
+            nc.vector.memset(plane[:].bitcast(I32), 0)
+            for q in range(4):
+                nc.sync.dma_start(
+                    plane[32 * q : 32 * q + 4, :].bitcast(I32), spread[32 * q : 32 * q + 32 : 8, :].bitcast(I32)
+                )
+            return plane
+
+        offs_sb = lists.tile([P, S // GROUP], U16, name="offs_sb")
+        take_sb = lists.tile([P, V // GROUP], U16, name="take_sb")
         nc.sync.dma_start(offs_sb[:], offs)
+
+        w1_rows = w1.rearrange("(p j) c -> p j c", j=SLOTS)
+        w1_raw = sb.tile([P, SLOTS, H], F32, name="w1_raw")
+        nc.sync.dma_start(w1_raw[:, :2, :], w1_rows[:, :2, :])
+        xs_table = load_scale_rows_spread(x_scales[0], "xs_table")
+        w2s_raw = load_scale_rows_spread(w2_scales[0], "w2s_raw")
+        nc.sync.dma_start(w1_raw[:, 2:, :], w1_rows[:, 2:, :])
+
+        x_table = sb.tile([P, T], U32, name="x_table", align_bytes=64)
+        nc.sync.dma_start(x_table[:].bitcast(I32), x_words[0].rearrange("p n t -> p (n t)").bitcast(I32))
+
+        xs_gathered = sb.tile([P, S], U8, name="xs_gathered", align_bytes=64)
+        nc.vector.tensor_copy(xs_gathered[:], xs_table[:].indirect(offs_sb[:]))
+        x_s = move_to_scale_rows(xs_gathered, "x_s")
+
+        w2_raw = sb.tile([P, 2 * N], U8, name="w2_raw", align_bytes=64)
+        nc.sync.dma_start(w2_raw[:].bitcast(I32), w2_words[0].bitcast(I32))
+        wt_sb = sb.tile([P, V], F32, name="wt_sb")
+        nc.sync.dma_start(wt_sb[:], wt.rearrange("(p j) v -> p j v", j=SLOTS)[:, 0, :])
         nc.sync.dma_start(take_sb[:], take)
 
-        w1_raw = sb.tile([P, PACK, H], F32, name="w1_raw", tag="w1_then_wt", align_bytes=64)
-        nc.sync.dma_start(w1_raw[:], w1.rearrange("(p j) c -> p j c", j=PACK))
-        x_tab = sb.tile([P, T], U32, name="x_tab", align_bytes=64)
-        nc.sync.dma_start(x_tab[:].bitcast(I32), x_words[0].rearrange("p n t -> p (n t)").bitcast(I32))
-
-        xs_tab = sb.tile([P, T], U8, name="xs_tab", tag="xs_then_w2", align_bytes=64)
-        nc.vector.memset(xs_tab[:].bitcast(I32), 0)
-        for q in range(4):
-            nc.scalar.dma_start(
-                xs_tab[32 * q : 32 * q + 4, :].bitcast(I32), x_scales[0, 4 * q : 4 * q + 4, :].bitcast(I32)
-            )
-        w2s_raw = sb.tile([P, N], U8, name="w2s_raw", align_bytes=64)
-        nc.gpsimd.memset(w2s_raw[:].bitcast(I32), 0)
-        for q in range(4):
-            nc.gpsimd.dma_start(
-                w2s_raw[32 * q : 32 * q + 4, :].bitcast(I32), w2_scales[0, 4 * q : 4 * q + 4, :].bitcast(I32)
-            )
-
-        z = [sb.tile([P, S], F32, name="z%d" % t) for t in range(PACK)]
-        for t in range(PACK):
+        z = [sb.tile([P, S], F32, name="z%d" % t) for t in range(SLOTS)]
+        for t in range(SLOTS):
             nc.vector.memset(z[t][:], 0.0)
-        warm = sb.tile([P, 1], F32, name="warm")
-        nc.scalar.activation(warm[:], z[0][:, 0:1], RELU)
 
-        xs_pick = sb.tile([P, S], U8, name="xs_pick", align_bytes=64)
-        nc.vector.tensor_copy(xs_pick[:], xs_tab[:].indirect(offs_sb[:]))
+        w1_bf = sb.tile([P, SLOTS * H], BF16, name="w1_bf", align_bytes=64)
+        for j in (0, 2):
+            nc.scalar.copy(
+                w1_bf[:].rearrange("p (t m j) -> p t m j", t=SLOTS, j=SLOTS)[:, :, :W1_SCALAR_M, j : j + 2],
+                w1_raw[:, j : j + 2, :].rearrange("p j (m t) -> p t m j", t=SLOTS)[:, :, :W1_SCALAR_M, :],
+            )
+        nc.vector.tensor_copy(
+            w1_bf[:].rearrange("p (t m j) -> p m t j", t=SLOTS, j=SLOTS)[:, W1_SCALAR_M:],
+            w1_raw[:].rearrange("p j (m t) -> p m t j", t=SLOTS)[:, W1_SCALAR_M:],
+        )
 
-        w1_bf = sb.tile([P, PACK * H], BF16, name="w1_bf", align_bytes=64)
-        w1_dst = w1_bf[:].rearrange("p (t m j) -> p m j t", t=PACK, j=PACK)
-        w1_src = w1_raw[:].rearrange("p j (m t) -> p m j t", t=PACK)
-        nc.scalar.copy(w1_dst[:, :SCALAR_M], w1_src[:, :SCALAR_M])
-        nc.vector.tensor_copy(w1_dst[:, SCALAR_M:], w1_src[:, SCALAR_M:])
+        w2s_dealt = sb.tile([P, N], U8, name="w2s_dealt", align_bytes=64)
+        nc.vector.tensor_copy(
+            w2s_dealt[:].rearrange("p (t g m) -> p g t m", t=SLOTS, m=16),
+            w2s_raw[:].rearrange("p (g m t) -> p g t m", t=SLOTS, m=16),
+        )
+        w2_s = move_to_scale_rows(w2s_dealt, "w2_s")
+
         w1_q = sb.tile([P, H], U32, name="w1_q", align_bytes=64)
         w1_s = sb.tile([P, H], U8, name="w1_s", align_bytes=64)
         nc.vector.quantize_mx(out=w1_q[:].bitcast(FP8X4), scales=w1_s[:], in_=w1_bf[:])
 
-        w2_raw = sb.tile([P, 2 * N], U8, name="w2_raw", tag="xs_then_w2", align_bytes=64)
-        nc.sync.dma_start(w2_raw[:].bitcast(I32), w2_words[0].bitcast(I32))
-        wt_sb = sb.tile([P, V], F32, name="wt_sb", tag="w1_then_wt", align_bytes=64)
-        nc.sync.dma_start(wt_sb[:], wt.rearrange("(p j) v -> p j v", j=PACK)[:, 0, :])
-
-        x_pick = sb.tile([P, S], U32, name="x_pick", align_bytes=64)
+        x_q = sb.tile([P, S], U32, name="x_q", align_bytes=64)
         for h in range(2):
-            nc.vector.tensor_copy(
-                x_pick[:, h * HALF : (h + 1) * HALF], x_tab[:].indirect(offs_sb[:, h * 16 : (h + 1) * 16])
-            )
+            entries = offs_sb[:, h * HALF // GROUP : (h + 1) * HALF // GROUP]
+            nc.vector.tensor_copy(x_q[:, h * HALF : (h + 1) * HALF], x_table[:].indirect(entries))
 
         w2_q = sb.tile([P, 2 * N], U8, name="w2_q", align_bytes=64)
-        w2_s = sb.tile([P, N], U8, name="w2_s", align_bytes=64)
         nc.vector.tensor_copy(
-            w2_s[:].rearrange("p (t m) -> p m t", t=PACK), w2s_raw[:].rearrange("p (m t) -> p m t", t=PACK)
-        )
-        nc.vector.tensor_copy(
-            w2_q[:].rearrange("p (t m b) -> p m t b", t=PACK, b=2),
-            w2_raw[:].rearrange("p (m t b) -> p m t b", t=PACK, b=2),
+            w2_q[:].rearrange("p (t g m b) -> p g t m b", t=SLOTS, m=8, b=2),
+            w2_raw[:].rearrange("p (g m t b) -> p g t m b", t=SLOTS, m=8, b=2),
         )
 
-        y = [sb.tile([P, S], F32, name="y%d" % t) for t in range(PACK)]
-
-        def first_layer(t, cols, bank):
-            width = cols.stop - cols.start
-            acc = psum.tile([P, width], F32, name="acc", tag="bank%d" % bank)
-            m_cols = slice(t * P, (t + 1) * P)
+        y = [sb.tile([P, S], F32, name="y%d" % t) for t in range(SLOTS)]
+        edges = [(0, HALF, HALF + CHUNK, S), (0, HALF, S), (0, S), (0, S)]
+        passes = [(t, slice(lo, hi)) for t in range(SLOTS) for lo, hi in zip(edges[t], edges[t][1:])]
+        y_accs = {}
+        for bank, (t, cols) in enumerate(sorted(passes, key=lambda item: item[1].stop > HALF)):
+            y_acc = psum.tile([P, cols.stop - cols.start], F32, name="y_acc", tag="bank%d" % bank)
             nc.tensor.matmul_mx(
-                out=acc[:],
-                lhsT=w1_q[:, m_cols].bitcast(FP8X4),
-                lhsT_scale=w1_s[:, m_cols],
-                rhs=x_pick[:, cols].bitcast(FP8X4),
-                rhs_scale=xs_pick[:, cols],
+                out=y_acc[:],
+                lhsT=w1_q[:, t * P : (t + 1) * P].bitcast(FP8X4),
+                lhsT_scale=w1_s[:, t * P : (t + 1) * P],
+                rhs=x_q[:, cols].bitcast(FP8X4),
+                rhs_scale=x_s[:, cols],
                 start=True,
                 stop=True,
             )
-            nc.scalar.activation(y[t][:, cols], acc[:], RELU)
+            y_accs[t, cols.start] = y_acc
+        for t, cols in passes:
+            nc.scalar.activation(y[t][:, cols], y_accs[t, cols.start][:], RELU)
 
-        first_layer(0, slice(0, HALF), 0)
-        first_layer(1, slice(0, HALF), 1)
-        first_layer(0, slice(HALF, S), 2)
-        first_layer(1, slice(HALF, S), 3)
-        first_layer(2, slice(0, S), 4)
-        first_layer(3, slice(0, S), 5)
-
-        e = [sb.tile([P, V], F32, name="e%d" % t) for t in range(PACK)]
-        z_bf = [sb.tile([P, CHUNK, PACK], BF16, name="z_bf%d" % c, align_bytes=64) for c in range(CHUNKS)]
+        taken = sb.tile([P, SLOTS, V], F32, name="taken")
+        z_bf = [sb.tile([P, CHUNK, SLOTS], BF16, name="z_bf%d" % c, align_bytes=64) for c in range(CHUNKS)]
 
         def gather(t):
-            nc.vector.tensor_copy(e[t][:], y[t][:].indirect(take_sb[:]))
+            nc.vector.tensor_copy(taken[:, t, :], y[t][:].indirect(take_sb[:]))
 
-        def scatter(t):
-            nc.vector.tensor_tensor(z[t][:].indirect(take_sb[:]), e[t][:], wt_sb[:], MULT)
-
-        def round_plane(t, c):
-            src = z[t][:, c * CHUNK : (c + 1) * CHUNK]
-            if t >= 2 and c == CHUNKS - 1:
-                nc.vector.tensor_copy(z_bf[c][:, :, t], src)
-            else:
-                nc.scalar.copy(z_bf[c][:, :, t], src)
+        def z_piece(t, c):
+            return z_bf[c][:, :, t], z[t][:, c * CHUNK : (c + 1) * CHUNK]
 
         gather(0)
-        for t in range(PACK):
-            if t + 1 < PACK:
+        for t in range(SLOTS):
+            if t + 1 < SLOTS:
                 gather(t + 1)
-            scatter(t)
-            for c in range(CHUNKS - 1):
-                round_plane(t, c)
-            if t < 2:
-                round_plane(t, CHUNKS - 1)
-        round_plane(2, CHUNKS - 1)
-        round_plane(3, CHUNKS - 1)
+            nc.vector.tensor_tensor(z[t][:].indirect(take_sb[:]), taken[:, t, :], wt_sb[:], MULT)
+            for c in range(CHUNKS):
+                if t < 2 or c != VECTOR_CHUNK:
+                    nc.scalar.copy(*z_piece(t, c))
+        for t in (2, 3):
+            nc.vector.tensor_copy(*z_piece(t, VECTOR_CHUNK))
 
         z_q = sb.tile([P, S], U32, name="z_q", align_bytes=64)
         z_s = sb.tile([P, S], U8, name="z_s", align_bytes=64)
+        spans = [slice(0, CHUNK), slice(CHUNK, S - CHUNK), slice(S - CHUNK, S)]
+        banks = []
+        for cols in spans:
+            width = cols.stop - cols.start
+            for c in range(cols.start // CHUNK, cols.stop // CHUNK):
+                chunk = slice(c * CHUNK, (c + 1) * CHUNK)
+                nc.vector.quantize_mx(
+                    out=z_q[:, chunk].bitcast(FP8X4),
+                    scales=z_s[:, chunk],
+                    in_=z_bf[c][:].rearrange("p n t -> p (n t)"),
+                )
+            planes_a_bank = 2 * CHUNK // width
+            for t0 in range(0, SLOTS, planes_a_bank):
+                o_acc = psum.tile([P, planes_a_bank, width], F32, name="o_acc", tag="bank%d" % len(banks))
+                for t in range(t0, t0 + planes_a_bank):
+                    nc.tensor.matmul_mx(
+                        out=o_acc[:, t - t0, :],
+                        lhsT=w2_q[:, 2 * t * P : 2 * (t + 1) * P].bitcast(FP4X4),
+                        lhsT_scale=w2_s[:, t * P : (t + 1) * P],
+                        rhs=z_q[:, cols].bitcast(FP8X4),
+                        rhs_scale=z_s[:, cols],
+                        start=True,
+                        stop=True,
+                    )
+                banks.append((cols, slice(t0, t0 + planes_a_bank), o_acc))
+
         o_q = sb.tile([P, S], U32, name="o_q", align_bytes=64)
         o_s = sb.tile([P, S], U8, name="o_s", align_bytes=64)
-        out_rows = out_0.rearrange("(p t) c -> p t c", t=PACK)
+        out_planes = out_0.rearrange("(p t) c -> p t c", t=SLOTS)
         out_words = out_1[0].rearrange("p n t -> p (n t)").bitcast(I32)
+        for i, cols in enumerate(spans):
+            width = cols.stop - cols.start
+            last = i == len(spans) - 1
+            o = sb.tile([P, SLOTS, width], F32, name="o%d" % i)
+            for bank_cols, planes, o_acc in banks:
+                if bank_cols == cols:
+                    nc.scalar.copy(o[:, planes, :], o_acc[:])
+                    if planes.stop % 2 == 0 and not last:
+                        pair = slice(planes.stop - 2, planes.stop)
+                        nc.sync.dma_start(out_planes[:, pair, cols], o[:, pair, :])
+            if last:
+                nc.sync.dma_start(out_planes[:, :, cols], o[:])
 
-        accs = []
-        for c in range(CHUNKS):
-            cols = slice(c * CHUNK, (c + 1) * CHUNK)
-            nc.vector.quantize_mx(
-                out=z_q[:, cols].bitcast(FP8X4), scales=z_s[:, cols], in_=z_bf[c][:].rearrange("p n t -> p (n t)")
-            )
-            acc = psum.tile([P, PACK, CHUNK], F32, name="acc2", tag="bank%d" % ((6 + c) % 8))
-            for t in range(PACK):
-                nc.tensor.matmul_mx(
-                    out=acc[:, t, :],
-                    lhsT=w2_q[:, 2 * t * P : 2 * (t + 1) * P].bitcast(FP4X4),
-                    lhsT_scale=w2_s[:, t * P : (t + 1) * P],
-                    rhs=z_q[:, cols].bitcast(FP8X4),
-                    rhs_scale=z_s[:, cols],
-                    start=True,
-                    stop=True,
-                )
-            accs.append(acc)
-
-        for c in range(CHUNKS):
-            cols = slice(c * CHUNK, (c + 1) * CHUNK)
-            o = sb.tile([P, PACK, CHUNK], F32, name="o%d" % c)
-            nc.scalar.copy(o[:], accs[c][:])
-            nc.sync.dma_start(out_rows[:, :, cols], o[:])
-            o_bf = sb.tile([P, CHUNK * PACK], BF16, name="o_bf%d" % c, align_bytes=64)
-            nc.vector.tensor_copy(
-                o_bf[:].rearrange("p (c i t) -> p c t i", i=4, t=PACK), o[:].rearrange("p t (c i) -> p c t i", i=4)
-            )
+            o_bf = sb.tile([P, width * SLOTS], BF16, name="o_bf%d" % i, align_bytes=64)
+            bf_dst = o_bf[:].rearrange("p (c n t) -> p c t n", n=4, t=SLOTS)
+            bf_src = o[:].rearrange("p t (c n) -> p c t n", n=4)
+            if last:
+                nc.scalar.copy(bf_dst[:, :LAST_SCALAR_GROUPS], bf_src[:, :LAST_SCALAR_GROUPS])
+                nc.vector.tensor_copy(bf_dst[:, LAST_SCALAR_GROUPS:], bf_src[:, LAST_SCALAR_GROUPS:])
+            else:
+                nc.vector.tensor_copy(bf_dst, bf_src)
             nc.vector.quantize_mx(out=o_q[:, cols].bitcast(FP8X4), scales=o_s[:, cols], in_=o_bf[:])
-            if c % 2 == 1:
-                both = slice((c - 1) * CHUNK, (c + 1) * CHUNK)
-                nc.sync.dma_start(out_words[:, both], o_q[:, both].bitcast(I32))
+            if i > 0:
+                done = cols if last else slice(0, cols.stop)
+                nc.sync.dma_start(out_words[:, done], o_q[:, done].bitcast(I32))
+
         for q in range(4):
             queue = nc.sync if q % 2 == 0 else nc.scalar
             queue.dma_start(out_2[0, 4 * q : 4 * q + 4, :].bitcast(I32), o_s[32 * q : 32 * q + 4, :].bitcast(I32))

@@ -135,7 +135,7 @@ def tile_picked_echoice_relu_po_kernel(
         z_bf = [sb.tile([P, CHUNK, SLOTS], BF16, name="z_bf%d" % c, align_bytes=64) for c in range(CHUNKS)]
 
         def gather(t):
-            nc.vector.tensor_copy(taken[:, t, :], y[t][:].indirect(take_sb[:]))
+            nc.vector.tensor_tensor(taken[:, t, :], y[t][:].indirect(take_sb[:]), wt_sb[:], MULT)
 
         def z_piece(t, c):
             return z_bf[c][:, :, t], z[t][:, c * CHUNK : (c + 1) * CHUNK]
@@ -144,7 +144,7 @@ def tile_picked_echoice_relu_po_kernel(
         for t in range(SLOTS):
             if t + 1 < SLOTS:
                 gather(t + 1)
-            nc.vector.tensor_tensor(z[t][:].indirect(take_sb[:]), taken[:, t, :], wt_sb[:], MULT)
+            nc.vector.tensor_copy(z[t][:].indirect(take_sb[:]), taken[:, t, :])
             for c in range(CHUNKS):
                 if t < 2 or c != VECTOR_CHUNK:
                     nc.scalar.copy(*z_piece(t, c))

@@ -21,8 +21,9 @@ HALF = S // 2
 CHUNK = 128
 CHUNKS = S // CHUNK
 W1_SCALAR_M = 56
-VECTOR_CHUNK = 1
-LAST_SCALAR_GROUPS = 12
+VECTOR_CHUNKS = 2
+BANKS = 8
+LAST_SCALAR_GROUPS = 24
 
 FLOPS = 2 * K * H * S + 2 * H * N * S
 
@@ -146,30 +147,52 @@ def tile_picked_echoice_relu_po_kernel(
                 gather(t + 1)
             nc.vector.tensor_copy(z[t][:].indirect(take_sb[:]), taken[:, t, :])
             for c in range(CHUNKS):
-                if t < 2 or c != VECTOR_CHUNK:
-                    nc.scalar.copy(*z_piece(t, c))
-        for t in (2, 3):
-            nc.vector.tensor_copy(*z_piece(t, VECTOR_CHUNK))
+                dst, src = z_piece(t, c)
+                if c >= VECTOR_CHUNKS or t < 2:
+                    nc.scalar.copy(dst, src)
+                elif t == 2:
+                    nc.scalar.copy(z_bf[c][:, :, 2:4], src.unsqueeze(2).to_broadcast([P, CHUNK, 2]))
+                else:
+                    nc.vector.tensor_copy(dst, src)
 
         z_q = sb.tile([P, S], U32, name="z_q", align_bytes=64)
         z_s = sb.tile([P, S], U8, name="z_s", align_bytes=64)
-        spans = [slice(0, CHUNK), slice(CHUNK, S - CHUNK), slice(S - CHUNK, S)]
-        banks = []
-        for cols in spans:
-            width = cols.stop - cols.start
-            for c in range(cols.start // CHUNK, cols.stop // CHUNK):
-                chunk = slice(c * CHUNK, (c + 1) * CHUNK)
-                nc.vector.quantize_mx(
-                    out=z_q[:, chunk].bitcast(FP8X4),
-                    scales=z_s[:, chunk],
-                    in_=z_bf[c][:].rearrange("p n t -> p (n t)"),
-                )
-            planes_a_bank = 2 * CHUNK // width
-            for t0 in range(0, SLOTS, planes_a_bank):
-                o_acc = psum.tile([P, planes_a_bank, width], F32, name="o_acc", tag="bank%d" % len(banks))
-                for t in range(t0, t0 + planes_a_bank):
+        for c in range(CHUNKS):
+            chunk = slice(c * CHUNK, (c + 1) * CHUNK)
+            nc.vector.quantize_mx(
+                out=z_q[:, chunk].bitcast(FP8X4),
+                scales=z_s[:, chunk],
+                in_=z_bf[c][:].rearrange("p n t -> p (n t)"),
+            )
+
+        first, second, third, last = (slice(c * CHUNK, (c + 1) * CHUNK) for c in range(CHUNKS))
+        jobs = [
+            ((0,), [first]),
+            ((1,), [first]),
+            ((2, 3), [first]),
+            ((0,), [second, slice(third.start, S)]),
+            ((1,), [second, slice(third.start, S)]),
+            ((2,), [slice(second.start, third.stop)]),
+            ((3,), [slice(second.start, third.stop)]),
+            ((2,), [last]),
+            ((3,), [last]),
+        ]
+        o_first = sb.tile([P, SLOTS, CHUNK], F32, name="o_first")
+        o_rest = sb.tile([P, SLOTS, S - CHUNK], F32, name="o_rest")
+        o_q = sb.tile([P, S], U32, name="o_q", align_bytes=64)
+        o_s = sb.tile([P, S], U8, name="o_s", align_bytes=64)
+        out_planes = out_0.rearrange("(p t) c -> p t c", t=SLOTS)
+        out_words = out_1[0].rearrange("p n t -> p (n t)").bitcast(I32)
+        rest = slice(CHUNK, S)
+
+        accs = []
+        for i, (planes, runs) in enumerate(jobs):
+            lo, hi = runs[0].start, runs[-1].stop
+            o_acc = psum.tile([P, len(planes), hi - lo], F32, name="o_acc", tag="bank%d" % (i % BANKS))
+            for k, t in enumerate(planes):
+                for cols in runs:
                     nc.tensor.matmul_mx(
-                        out=o_acc[:, t - t0, :],
+                        out=o_acc[:, k, cols.start - lo : cols.stop - lo],
                         lhsT=w2_q[:, 2 * t * P : 2 * (t + 1) * P].bitcast(FP4X4),
                         lhsT_scale=w2_s[:, t * P : (t + 1) * P],
                         rhs=z_q[:, cols].bitcast(FP8X4),
@@ -177,37 +200,49 @@ def tile_picked_echoice_relu_po_kernel(
                         start=True,
                         stop=True,
                     )
-                banks.append((cols, slice(t0, t0 + planes_a_bank), o_acc))
+            accs.append(o_acc)
+            if i == 0:
+                nc.scalar.copy(o_first[:, 0:1, :], o_acc[:])
+                nc.sync.dma_start(out_planes[:, 0:1, first], o_first[:, 0:1, :])
 
-        o_q = sb.tile([P, S], U32, name="o_q", align_bytes=64)
-        o_s = sb.tile([P, S], U8, name="o_s", align_bytes=64)
-        out_planes = out_0.rearrange("(p t) c -> p t c", t=SLOTS)
-        out_words = out_1[0].rearrange("p n t -> p (n t)").bitcast(I32)
-        for i, cols in enumerate(spans):
-            width = cols.stop - cols.start
-            last = i == len(spans) - 1
-            o = sb.tile([P, SLOTS, width], F32, name="o%d" % i)
-            for bank_cols, planes, o_acc in banks:
-                if bank_cols == cols:
-                    nc.scalar.copy(o[:, planes, :], o_acc[:])
-                    if planes.stop % 2 == 0 and not last:
-                        pair = slice(planes.stop - 2, planes.stop)
-                        nc.sync.dma_start(out_planes[:, pair, cols], o[:, pair, :])
-            if last:
-                nc.sync.dma_start(out_planes[:, :, cols], o[:])
+        def empty(i, engine_copy):
+            planes, runs = jobs[i]
+            lo, hi = runs[0].start, runs[-1].stop
+            held = slice(planes[0], planes[-1] + 1)
+            dst = o_first[:, held, :] if lo == 0 else o_rest[:, held, lo - CHUNK : hi - CHUNK]
+            engine_copy(dst, accs[i][:])
 
-            o_bf = sb.tile([P, width * SLOTS], BF16, name="o_bf%d" % i, align_bytes=64)
-            bf_dst = o_bf[:].rearrange("p (c n t) -> p c t n", n=4, t=SLOTS)
-            bf_src = o[:].rearrange("p t (c n) -> p c t n", n=4)
-            if last:
-                nc.scalar.copy(bf_dst[:, :LAST_SCALAR_GROUPS], bf_src[:, :LAST_SCALAR_GROUPS])
-                nc.vector.tensor_copy(bf_dst[:, LAST_SCALAR_GROUPS:], bf_src[:, LAST_SCALAR_GROUPS:])
-            else:
-                nc.vector.tensor_copy(bf_dst, bf_src)
-            nc.vector.quantize_mx(out=o_q[:, cols].bitcast(FP8X4), scales=o_s[:, cols], in_=o_bf[:])
-            if i > 0:
-                done = cols if last else slice(0, cols.stop)
-                nc.sync.dma_start(out_words[:, done], o_q[:, done].bitcast(I32))
+        def round_groups(engine_copy, dst, src, lo, hi):
+            engine_copy(
+                dst.rearrange("p (c n t) -> p c t n", n=4, t=SLOTS)[:, lo:hi],
+                src.rearrange("p t (c n) -> p c t n", n=4)[:, lo:hi],
+            )
+
+        groups = CHUNK // 4
+        for i, held in ((1, slice(1, 2)), (2, slice(2, 4))):
+            empty(i, nc.scalar.copy)
+            nc.sync.dma_start(out_planes[:, held, first], o_first[:, held, :])
+        bf_first = sb.tile([P, CHUNK * SLOTS], BF16, name="bf_first", align_bytes=64)
+        round_groups(nc.vector.tensor_copy, bf_first[:], o_first[:], 0, groups)
+        empty(3, nc.scalar.copy)
+        nc.sync.dma_start(out_planes[:, 0, rest], o_rest[:, 0, :])
+        empty(4, nc.vector.tensor_copy)
+        nc.sync.dma_start(out_planes[:, 1, rest], o_rest[:, 1, :])
+        nc.vector.quantize_mx(out=o_q[:, first].bitcast(FP8X4), scales=o_s[:, first], in_=bf_first[:])
+        nc.sync.dma_start(out_words[:, first], o_q[:, first].bitcast(I32))
+        for i in range(5, len(jobs)):
+            empty(i, nc.scalar.copy)
+        nc.sync.dma_start(out_planes[:, 2:4, rest], o_rest[:, 2:4, :])
+
+        middle = slice(second.start, third.stop)
+        bf_middle = sb.tile([P, 2 * CHUNK * SLOTS], BF16, name="bf_middle", align_bytes=64)
+        bf_last = sb.tile([P, CHUNK * SLOTS], BF16, name="bf_last", align_bytes=64)
+        round_groups(nc.vector.tensor_copy, bf_middle[:], o_rest[:, :, : 2 * CHUNK], 0, 2 * groups)
+        round_groups(nc.scalar.copy, bf_last[:], o_rest[:, :, 2 * CHUNK :], 0, LAST_SCALAR_GROUPS)
+        round_groups(nc.vector.tensor_copy, bf_last[:], o_rest[:, :, 2 * CHUNK :], LAST_SCALAR_GROUPS, groups)
+        nc.vector.quantize_mx(out=o_q[:, middle].bitcast(FP8X4), scales=o_s[:, middle], in_=bf_middle[:])
+        nc.vector.quantize_mx(out=o_q[:, last].bitcast(FP8X4), scales=o_s[:, last], in_=bf_last[:])
+        nc.sync.dma_start(out_words[:, rest], o_q[:, rest].bitcast(I32))
 
         for q in range(4):
             queue = nc.sync if q % 2 == 0 else nc.scalar

@@ -23,7 +23,7 @@ CHUNKS = S // CHUNK
 W1_SCALAR_M = 56
 VECTOR_CHUNKS = 2
 BANKS = 8
-LAST_SCALAR_GROUPS = 24
+SCALAR_GROUPS = 8
 
 FLOPS = 2 * K * H * S + 2 * H * N * S
 
@@ -54,11 +54,11 @@ def tile_picked_echoice_relu_po_kernel(
 
         offs_sb = lists.tile([P, S // GROUP], U16, name="offs_sb")
         take_sb = lists.tile([P, V // GROUP], U16, name="take_sb")
-        nc.sync.dma_start(offs_sb[:], offs)
 
         w1_rows = w1.rearrange("(p j) c -> p j c", j=SLOTS)
         w1_raw = sb.tile([P, SLOTS, H], F32, name="w1_raw")
         nc.sync.dma_start(w1_raw[:, :2, :], w1_rows[:, :2, :])
+        nc.sync.dma_start(offs_sb[:], offs)
         xs_table = load_scale_rows_spread(x_scales[0], "xs_table")
         w2s_raw = load_scale_rows_spread(w2_scales[0], "w2s_raw")
         nc.sync.dma_start(w1_raw[:, 2:, :], w1_rows[:, 2:, :])
@@ -165,34 +165,31 @@ def tile_picked_echoice_relu_po_kernel(
                 in_=z_bf[c][:].rearrange("p n t -> p (n t)"),
             )
 
-        first, second, third, last = (slice(c * CHUNK, (c + 1) * CHUNK) for c in range(CHUNKS))
-        jobs = [
-            ((0,), [first]),
-            ((1,), [first]),
-            ((2, 3), [first]),
-            ((0,), [second, slice(third.start, S)]),
-            ((1,), [second, slice(third.start, S)]),
-            ((2,), [slice(second.start, third.stop)]),
-            ((3,), [slice(second.start, third.stop)]),
-            ((2,), [last]),
-            ((3,), [last]),
-        ]
-        o_first = sb.tile([P, SLOTS, CHUNK], F32, name="o_first")
-        o_rest = sb.tile([P, SLOTS, S - CHUNK], F32, name="o_rest")
         o_q = sb.tile([P, S], U32, name="o_q", align_bytes=64)
         o_s = sb.tile([P, S], U8, name="o_s", align_bytes=64)
         out_planes = out_0.rearrange("(p t) c -> p t c", t=SLOTS)
         out_words = out_1[0].rearrange("p n t -> p (n t)").bitcast(I32)
-        rest = slice(CHUNK, S)
+        banks_used = 0
+        rounded = []
+        scalar_shares = []
 
-        accs = []
-        for i, (planes, runs) in enumerate(jobs):
-            lo, hi = runs[0].start, runs[-1].stop
-            o_acc = psum.tile([P, len(planes), hi - lo], F32, name="o_acc", tag="bank%d" % (i % BANKS))
-            for k, t in enumerate(planes):
-                for cols in runs:
+        def quantise_out(c):
+            cols, o_bf = rounded[c]
+            nc.vector.quantize_mx(out=o_q[:, cols].bitcast(FP8X4), scales=o_s[:, cols], in_=o_bf[:])
+            if c >= CHUNKS - 2:
+                done = cols if c == CHUNKS - 1 else slice(0, cols.stop)
+                nc.sync.dma_start(out_words[:, done], o_q[:, done].bitcast(I32))
+
+        for c in range(CHUNKS):
+            cols = slice(c * CHUNK, (c + 1) * CHUNK)
+            last = c == CHUNKS - 1
+            o = sb.tile([P, SLOTS, CHUNK], F32, name="o%d" % c)
+            for planes in [(0, 1), (2,), (3,)] if last else [(0, 1), (2, 3)]:
+                o_acc = psum.tile([P, len(planes), CHUNK], F32, name="o_acc", tag="bank%d" % (banks_used % BANKS))
+                banks_used = banks_used + 1
+                for k, t in enumerate(planes):
                     nc.tensor.matmul_mx(
-                        out=o_acc[:, k, cols.start - lo : cols.stop - lo],
+                        out=o_acc[:, k, :],
                         lhsT=w2_q[:, 2 * t * P : 2 * (t + 1) * P].bitcast(FP4X4),
                         lhsT_scale=w2_s[:, t * P : (t + 1) * P],
                         rhs=z_q[:, cols].bitcast(FP8X4),
@@ -200,49 +197,24 @@ def tile_picked_echoice_relu_po_kernel(
                         start=True,
                         stop=True,
                     )
-            accs.append(o_acc)
-            if i == 0:
-                nc.scalar.copy(o_first[:, 0:1, :], o_acc[:])
-                nc.sync.dma_start(out_planes[:, 0:1, first], o_first[:, 0:1, :])
+                copy_out = nc.vector.tensor_copy if banks_used == 1 else nc.scalar.copy
+                copy_out(o[:, planes[0] : planes[-1] + 1, :], o_acc[:])
+            nc.sync.dma_start(out_planes[:, :, cols], o[:])
 
-        def empty(i, engine_copy):
-            planes, runs = jobs[i]
-            lo, hi = runs[0].start, runs[-1].stop
-            held = slice(planes[0], planes[-1] + 1)
-            dst = o_first[:, held, :] if lo == 0 else o_rest[:, held, lo - CHUNK : hi - CHUNK]
-            engine_copy(dst, accs[i][:])
-
-        def round_groups(engine_copy, dst, src, lo, hi):
-            engine_copy(
-                dst.rearrange("p (c n t) -> p c t n", n=4, t=SLOTS)[:, lo:hi],
-                src.rearrange("p t (c n) -> p c t n", n=4)[:, lo:hi],
-            )
-
-        groups = CHUNK // 4
-        for i, held in ((1, slice(1, 2)), (2, slice(2, 4))):
-            empty(i, nc.scalar.copy)
-            nc.sync.dma_start(out_planes[:, held, first], o_first[:, held, :])
-        bf_first = sb.tile([P, CHUNK * SLOTS], BF16, name="bf_first", align_bytes=64)
-        round_groups(nc.vector.tensor_copy, bf_first[:], o_first[:], 0, groups)
-        empty(3, nc.scalar.copy)
-        nc.sync.dma_start(out_planes[:, 0, rest], o_rest[:, 0, :])
-        empty(4, nc.vector.tensor_copy)
-        nc.sync.dma_start(out_planes[:, 1, rest], o_rest[:, 1, :])
-        nc.vector.quantize_mx(out=o_q[:, first].bitcast(FP8X4), scales=o_s[:, first], in_=bf_first[:])
-        nc.sync.dma_start(out_words[:, first], o_q[:, first].bitcast(I32))
-        for i in range(5, len(jobs)):
-            empty(i, nc.scalar.copy)
-        nc.sync.dma_start(out_planes[:, 2:4, rest], o_rest[:, 2:4, :])
-
-        middle = slice(second.start, third.stop)
-        bf_middle = sb.tile([P, 2 * CHUNK * SLOTS], BF16, name="bf_middle", align_bytes=64)
-        bf_last = sb.tile([P, CHUNK * SLOTS], BF16, name="bf_last", align_bytes=64)
-        round_groups(nc.vector.tensor_copy, bf_middle[:], o_rest[:, :, : 2 * CHUNK], 0, 2 * groups)
-        round_groups(nc.scalar.copy, bf_last[:], o_rest[:, :, 2 * CHUNK :], 0, LAST_SCALAR_GROUPS)
-        round_groups(nc.vector.tensor_copy, bf_last[:], o_rest[:, :, 2 * CHUNK :], LAST_SCALAR_GROUPS, groups)
-        nc.vector.quantize_mx(out=o_q[:, middle].bitcast(FP8X4), scales=o_s[:, middle], in_=bf_middle[:])
-        nc.vector.quantize_mx(out=o_q[:, last].bitcast(FP8X4), scales=o_s[:, last], in_=bf_last[:])
-        nc.sync.dma_start(out_words[:, rest], o_q[:, rest].bitcast(I32))
+            o_bf = sb.tile([P, CHUNK * SLOTS], BF16, name="o_bf%d" % c, align_bytes=64)
+            bf_dst = o_bf[:].rearrange("p (c n t) -> p c t n", n=4, t=SLOTS)
+            bf_src = o[:].rearrange("p t (c n) -> p c t n", n=4)
+            if c >= CHUNKS - 2:
+                nc.vector.tensor_copy(bf_dst[:, SCALAR_GROUPS:], bf_src[:, SCALAR_GROUPS:])
+                scalar_shares.append((bf_dst[:, :SCALAR_GROUPS], bf_src[:, :SCALAR_GROUPS]))
+            else:
+                nc.vector.tensor_copy(bf_dst, bf_src)
+            rounded.append((cols, o_bf))
+            if 0 < c < CHUNKS - 1:
+                quantise_out(c - 1)
+        for c, share in zip(range(CHUNKS - 2, CHUNKS), scalar_shares):
+            nc.scalar.copy(*share)
+            quantise_out(c)
 
         for q in range(4):
             queue = nc.sync if q % 2 == 0 else nc.scalar

@@ -11,6 +11,7 @@ U8 = mybir.dt.uint8
 FP8X4 = mybir.dt.float8_e4m3fn_x4
 FP4X4 = mybir.dt.float4_e2m1fn_x4
 RELU = mybir.ActivationFunctionType.Relu
+IDENTITY = mybir.ActivationFunctionType.Identity
 MULT = mybir.AluOpType.mult
 
 P = 128
@@ -23,7 +24,8 @@ CHUNKS = S // CHUNK
 W1_SCALAR_M = 56
 VECTOR_CHUNKS = 2
 BANKS = 8
-SCALAR_GROUPS = 8
+WARM_AFTER = (1, 0)
+SCALAR_GROUPS = 12
 
 FLOPS = 2 * K * H * S + 2 * H * N * S
 
@@ -60,7 +62,6 @@ def tile_picked_echoice_relu_po_kernel(
         nc.sync.dma_start(w1_raw[:, :2, :], w1_rows[:, :2, :])
         nc.sync.dma_start(offs_sb[:], offs)
         xs_table = load_scale_rows_spread(x_scales[0], "xs_table")
-        w2s_raw = load_scale_rows_spread(w2_scales[0], "w2s_raw")
         nc.sync.dma_start(w1_raw[:, 2:, :], w1_rows[:, 2:, :])
 
         x_table = sb.tile([P, T], U32, name="x_table", align_bytes=64)
@@ -70,6 +71,7 @@ def tile_picked_echoice_relu_po_kernel(
         nc.vector.tensor_copy(xs_gathered[:], xs_table[:].indirect(offs_sb[:]))
         x_s = move_to_scale_rows(xs_gathered, "x_s")
 
+        w2s_raw = load_scale_rows_spread(w2_scales[0], "w2s_raw")
         w2_raw = sb.tile([P, 2 * N], U8, name="w2_raw", align_bytes=64)
         nc.sync.dma_start(w2_raw[:].bitcast(I32), w2_words[0].bitcast(I32))
         wt_sb = sb.tile([P, V], F32, name="wt_sb")
@@ -91,13 +93,6 @@ def tile_picked_echoice_relu_po_kernel(
             w1_raw[:].rearrange("p j (m t) -> p m t j", t=SLOTS)[:, W1_SCALAR_M:],
         )
 
-        w2s_dealt = sb.tile([P, N], U8, name="w2s_dealt", align_bytes=64)
-        nc.vector.tensor_copy(
-            w2s_dealt[:].rearrange("p (t g m) -> p g t m", t=SLOTS, m=16),
-            w2s_raw[:].rearrange("p (g m t) -> p g t m", t=SLOTS, m=16),
-        )
-        w2_s = move_to_scale_rows(w2s_dealt, "w2_s")
-
         w1_q = sb.tile([P, H], U32, name="w1_q", align_bytes=64)
         w1_s = sb.tile([P, H], U8, name="w1_s", align_bytes=64)
         nc.vector.quantize_mx(out=w1_q[:].bitcast(FP8X4), scales=w1_s[:], in_=w1_bf[:])
@@ -112,6 +107,14 @@ def tile_picked_echoice_relu_po_kernel(
             w2_q[:].rearrange("p (t g m b) -> p g t m b", t=SLOTS, m=8, b=2),
             w2_raw[:].rearrange("p (g m t b) -> p g t m b", t=SLOTS, m=8, b=2),
         )
+
+        w2s_dealt = sb.tile([P, N], U8, name="w2s_dealt", align_bytes=64)
+        nc.vector.tensor_copy(
+            w2s_dealt[:].rearrange("p (t g m) -> p g t m", t=SLOTS, m=16),
+            w2s_raw[:].rearrange("p (g m t) -> p g t m", t=SLOTS, m=16),
+        )
+        w2_s = sb.tile([P, N], U8, name="w2_s", align_bytes=64)
+        nc.vector.memset(w2_s[:].bitcast(I32), 0)
 
         y = [sb.tile([P, S], F32, name="y%d" % t) for t in range(SLOTS)]
         edges = [(0, HALF, HALF + CHUNK, S), (0, HALF, S), (0, S), (0, S)]
@@ -148,7 +151,25 @@ def tile_picked_echoice_relu_po_kernel(
             nc.vector.tensor_copy(z[t][:].indirect(take_sb[:]), taken[:, t, :])
             for c in range(CHUNKS):
                 dst, src = z_piece(t, c)
-                if c >= VECTOR_CHUNKS or t < 2:
+                if (t, c) == WARM_AFTER:
+                    nc.scalar.activation(dst, src, IDENTITY, bias=w2_s[:, 0:4].bitcast(F32))
+                    for q in range(4):
+                        nc.sync.dma_start(
+                            w2_s[32 * q : 32 * q + 4, :].bitcast(I32),
+                            w2s_dealt[32 * q : 32 * q + 32 : 8, :].bitcast(I32),
+                        )
+                    for k in range(2):
+                        spare = psum.tile([P, S], F32, name="spare", tag="bank%d" % (BANKS - 1 - k))
+                        nc.tensor.matmul_mx(
+                            out=spare[:],
+                            lhsT=w2_q[:, : 2 * P].bitcast(FP4X4),
+                            lhsT_scale=w2_s[:, :P],
+                            rhs=x_q[:].bitcast(FP8X4),
+                            rhs_scale=x_s[:],
+                            start=True,
+                            stop=True,
+                        )
+                elif c >= VECTOR_CHUNKS or t < 2:
                     nc.scalar.copy(dst, src)
                 elif t == 2:
                     nc.scalar.copy(z_bf[c][:, :, 2:4], src.unsqueeze(2).to_broadcast([P, CHUNK, 2]))
@@ -176,9 +197,9 @@ def tile_picked_echoice_relu_po_kernel(
         def quantise_out(c):
             cols, o_bf = rounded[c]
             nc.vector.quantize_mx(out=o_q[:, cols].bitcast(FP8X4), scales=o_s[:, cols], in_=o_bf[:])
-            if c >= CHUNKS - 2:
-                done = cols if c == CHUNKS - 1 else slice(0, cols.stop)
-                nc.sync.dma_start(out_words[:, done], o_q[:, done].bitcast(I32))
+            if c % 2 == 1:
+                half = slice(cols.stop - HALF, cols.stop)
+                nc.sync.dma_start(out_words[:, half], o_q[:, half].bitcast(I32))
 
         for c in range(CHUNKS):
             cols = slice(c * CHUNK, (c + 1) * CHUNK)
@@ -197,9 +218,13 @@ def tile_picked_echoice_relu_po_kernel(
                         start=True,
                         stop=True,
                     )
-                copy_out = nc.vector.tensor_copy if banks_used == 1 else nc.scalar.copy
-                copy_out(o[:, planes[0] : planes[-1] + 1, :], o_acc[:])
-            nc.sync.dma_start(out_planes[:, :, cols], o[:])
+                copy_out = nc.vector.tensor_copy if banks_used in (2, 3) else nc.scalar.copy
+                held = slice(planes[0], planes[-1] + 1)
+                copy_out(o[:, held, :], o_acc[:])
+                if c == 0:
+                    nc.sync.dma_start(out_planes[:, held, cols], o[:, held, :])
+            if c > 0:
+                nc.sync.dma_start(out_planes[:, :, cols], o[:])
 
             o_bf = sb.tile([P, CHUNK * SLOTS], BF16, name="o_bf%d" % c, align_bytes=64)
             bf_dst = o_bf[:].rearrange("p (c n t) -> p c t n", n=4, t=SLOTS)

@@ -24,7 +24,8 @@ CHUNKS = S // CHUNK
 W1_SCALAR_M = 56
 VECTOR_CHUNKS = 2
 BANKS = 8
-WARM_AFTER = (1, 0)
+WARM_UPS = 2
+LEAD = 16
 SCALAR_GROUPS = 12
 
 FLOPS = 2 * K * H * S + 2 * H * N * S
@@ -45,14 +46,16 @@ def tile_picked_echoice_relu_po_kernel(
             nc.sync.dma_start(spread[0:P:8, :].bitcast(I32), rows.bitcast(I32))
             return spread
 
-        def move_to_scale_rows(spread, name):
-            plane = sb.tile([P, spread.shape[1]], U8, name=name, align_bytes=64)
-            nc.vector.memset(plane[:].bitcast(I32), 0)
+        def zeroed_scales(columns, name):
+            scales = sb.tile([P, columns], U8, name=name, align_bytes=64)
+            nc.vector.memset(scales[:].bitcast(I32), 0)
+            return scales
+
+        def move_to_scale_rows(spread, scales):
             for q in range(4):
                 nc.sync.dma_start(
-                    plane[32 * q : 32 * q + 4, :].bitcast(I32), spread[32 * q : 32 * q + 32 : 8, :].bitcast(I32)
+                    scales[32 * q : 32 * q + 4, :].bitcast(I32), spread[32 * q : 32 * q + 32 : 8, :].bitcast(I32)
                 )
-            return plane
 
         offs_sb = lists.tile([P, S // GROUP], U16, name="offs_sb")
         take_sb = lists.tile([P, V // GROUP], U16, name="take_sb")
@@ -69,7 +72,8 @@ def tile_picked_echoice_relu_po_kernel(
 
         xs_gathered = sb.tile([P, S], U8, name="xs_gathered", align_bytes=64)
         nc.vector.tensor_copy(xs_gathered[:], xs_table[:].indirect(offs_sb[:]))
-        x_s = move_to_scale_rows(xs_gathered, "x_s")
+        x_s = zeroed_scales(S, "x_s")
+        move_to_scale_rows(xs_gathered, x_s)
 
         w2s_raw = load_scale_rows_spread(w2_scales[0], "w2s_raw")
         w2_raw = sb.tile([P, 2 * N], U8, name="w2_raw", align_bytes=64)
@@ -113,8 +117,7 @@ def tile_picked_echoice_relu_po_kernel(
             w2s_dealt[:].rearrange("p (t g m) -> p g t m", t=SLOTS, m=16),
             w2s_raw[:].rearrange("p (g m t) -> p g t m", t=SLOTS, m=16),
         )
-        w2_s = sb.tile([P, N], U8, name="w2_s", align_bytes=64)
-        nc.vector.memset(w2_s[:].bitcast(I32), 0)
+        w2_s = zeroed_scales(N, "w2_s")
 
         y = [sb.tile([P, S], F32, name="y%d" % t) for t in range(SLOTS)]
         edges = [(0, HALF, HALF + CHUNK, S), (0, HALF, S), (0, S), (0, S)]
@@ -144,6 +147,21 @@ def tile_picked_echoice_relu_po_kernel(
         def z_piece(t, c):
             return z_bf[c][:, :, t], z[t][:, c * CHUNK : (c + 1) * CHUNK]
 
+        def release_warm_up(dst, src):
+            nc.scalar.activation(dst, src, IDENTITY, bias=w2_s[:, 0:4].bitcast(F32))
+            move_to_scale_rows(w2s_dealt, w2_s)
+            for i in range(WARM_UPS):
+                spare = psum.tile([P, S], F32, name="spare", tag="bank%d" % (BANKS - 1 - i))
+                nc.tensor.matmul_mx(
+                    out=spare[:],
+                    lhsT=w2_q[:, : 2 * P].bitcast(FP4X4),
+                    lhsT_scale=w2_s[:, :P],
+                    rhs=x_q[:].bitcast(FP8X4),
+                    rhs_scale=x_s[:],
+                    start=True,
+                    stop=True,
+                )
+
         gather(0)
         for t in range(SLOTS):
             if t + 1 < SLOTS:
@@ -151,24 +169,9 @@ def tile_picked_echoice_relu_po_kernel(
             nc.vector.tensor_copy(z[t][:].indirect(take_sb[:]), taken[:, t, :])
             for c in range(CHUNKS):
                 dst, src = z_piece(t, c)
-                if (t, c) == WARM_AFTER:
-                    nc.scalar.activation(dst, src, IDENTITY, bias=w2_s[:, 0:4].bitcast(F32))
-                    for q in range(4):
-                        nc.sync.dma_start(
-                            w2_s[32 * q : 32 * q + 4, :].bitcast(I32),
-                            w2s_dealt[32 * q : 32 * q + 32 : 8, :].bitcast(I32),
-                        )
-                    for k in range(2):
-                        spare = psum.tile([P, S], F32, name="spare", tag="bank%d" % (BANKS - 1 - k))
-                        nc.tensor.matmul_mx(
-                            out=spare[:],
-                            lhsT=w2_q[:, : 2 * P].bitcast(FP4X4),
-                            lhsT_scale=w2_s[:, :P],
-                            rhs=x_q[:].bitcast(FP8X4),
-                            rhs_scale=x_s[:],
-                            start=True,
-                            stop=True,
-                        )
+                if (t, c) == (1, 0):
+                    release_warm_up(dst[:, :LEAD], src[:, :LEAD])
+                    nc.scalar.copy(dst[:, LEAD:], src[:, LEAD:])
                 elif c >= VECTOR_CHUNKS or t < 2:
                     nc.scalar.copy(dst, src)
                 elif t == 2:
@@ -205,12 +208,13 @@ def tile_picked_echoice_relu_po_kernel(
             cols = slice(c * CHUNK, (c + 1) * CHUNK)
             last = c == CHUNKS - 1
             o = sb.tile([P, SLOTS, CHUNK], F32, name="o%d" % c)
-            for planes in [(0, 1), (2,), (3,)] if last else [(0, 1), (2, 3)]:
+            by_bank = [(0,), (1,), (2, 3)] if c == 0 else [(0, 1), (2,), (3,)] if last else [(0, 1), (2, 3)]
+            for planes in by_bank:
                 o_acc = psum.tile([P, len(planes), CHUNK], F32, name="o_acc", tag="bank%d" % (banks_used % BANKS))
                 banks_used = banks_used + 1
-                for k, t in enumerate(planes):
+                for place, t in enumerate(planes):
                     nc.tensor.matmul_mx(
-                        out=o_acc[:, k, :],
+                        out=o_acc[:, place, :],
                         lhsT=w2_q[:, 2 * t * P : 2 * (t + 1) * P].bitcast(FP4X4),
                         lhsT_scale=w2_s[:, t * P : (t + 1) * P],
                         rhs=z_q[:, cols].bitcast(FP8X4),
@@ -218,17 +222,18 @@ def tile_picked_echoice_relu_po_kernel(
                         start=True,
                         stop=True,
                     )
-                copy_out = nc.vector.tensor_copy if banks_used in (2, 3) else nc.scalar.copy
+                on_vector = (c, planes) in ((0, (2, 3)), (1, (0, 1)))
+                copy_out = nc.vector.tensor_copy if on_vector else nc.scalar.copy
                 held = slice(planes[0], planes[-1] + 1)
                 copy_out(o[:, held, :], o_acc[:])
-                if c == 0:
+                if cols.stop <= HALF:
                     nc.sync.dma_start(out_planes[:, held, cols], o[:, held, :])
-            if c > 0:
+            if cols.stop > HALF:
                 nc.sync.dma_start(out_planes[:, :, cols], o[:])
 
             o_bf = sb.tile([P, CHUNK * SLOTS], BF16, name="o_bf%d" % c, align_bytes=64)
-            bf_dst = o_bf[:].rearrange("p (c n t) -> p c t n", n=4, t=SLOTS)
-            bf_src = o[:].rearrange("p t (c n) -> p c t n", n=4)
+            bf_dst = o_bf[:].rearrange("p (g n t) -> p g t n", n=4, t=SLOTS)
+            bf_src = o[:].rearrange("p t (g n) -> p g t n", n=4)
             if c >= CHUNKS - 2:
                 nc.vector.tensor_copy(bf_dst[:, SCALAR_GROUPS:], bf_src[:, SCALAR_GROUPS:])
                 scalar_shares.append((bf_dst[:, :SCALAR_GROUPS], bf_src[:, :SCALAR_GROUPS]))

@@ -11,7 +11,6 @@ U8 = mybir.dt.uint8
 FP8X4 = mybir.dt.float8_e4m3fn_x4
 FP4X4 = mybir.dt.float4_e2m1fn_x4
 RELU = mybir.ActivationFunctionType.Relu
-IDENTITY = mybir.ActivationFunctionType.Identity
 MULT = mybir.AluOpType.mult
 
 P = 128
@@ -24,8 +23,6 @@ CHUNKS = S // CHUNK
 W1_SCALAR_M = 56
 VECTOR_CHUNKS = 2
 BANKS = 8
-WARM_UPS = 2
-LEAD = 16
 SCALAR_GROUPS = 12
 
 FLOPS = 2 * K * H * S + 2 * H * N * S
@@ -118,6 +115,7 @@ def tile_picked_echoice_relu_po_kernel(
             w2s_raw[:].rearrange("p (g m t) -> p g t m", t=SLOTS, m=16),
         )
         w2_s = zeroed_scales(N, "w2_s")
+        move_to_scale_rows(w2s_dealt, w2_s)
 
         y = [sb.tile([P, S], F32, name="y%d" % t) for t in range(SLOTS)]
         edges = [(0, HALF, HALF + CHUNK, S), (0, HALF, S), (0, S), (0, S)]
@@ -147,21 +145,6 @@ def tile_picked_echoice_relu_po_kernel(
         def z_piece(t, c):
             return z_bf[c][:, :, t], z[t][:, c * CHUNK : (c + 1) * CHUNK]
 
-        def release_warm_up(dst, src):
-            nc.scalar.activation(dst, src, IDENTITY, bias=w2_s[:, 0:4].bitcast(F32))
-            move_to_scale_rows(w2s_dealt, w2_s)
-            for i in range(WARM_UPS):
-                spare = psum.tile([P, S], F32, name="spare", tag="bank%d" % (BANKS - 1 - i))
-                nc.tensor.matmul_mx(
-                    out=spare[:],
-                    lhsT=w2_q[:, : 2 * P].bitcast(FP4X4),
-                    lhsT_scale=w2_s[:, :P],
-                    rhs=x_q[:].bitcast(FP8X4),
-                    rhs_scale=x_s[:],
-                    start=True,
-                    stop=True,
-                )
-
         gather(0)
         for t in range(SLOTS):
             if t + 1 < SLOTS:
@@ -169,10 +152,7 @@ def tile_picked_echoice_relu_po_kernel(
             nc.vector.tensor_copy(z[t][:].indirect(take_sb[:]), taken[:, t, :])
             for c in range(CHUNKS):
                 dst, src = z_piece(t, c)
-                if (t, c) == (1, 0):
-                    release_warm_up(dst[:, :LEAD], src[:, :LEAD])
-                    nc.scalar.copy(dst[:, LEAD:], src[:, LEAD:])
-                elif c >= VECTOR_CHUNKS or t < 2:
+                if c >= VECTOR_CHUNKS or t < 2:
                     nc.scalar.copy(dst, src)
                 elif t == 2:
                     nc.scalar.copy(z_bf[c][:, :, 2:4], src.unsqueeze(2).to_broadcast([P, CHUNK, 2]))

@@ -11,6 +11,7 @@ U8 = mybir.dt.uint8
 FP8X4 = mybir.dt.float8_e4m3fn_x4
 FP4X4 = mybir.dt.float4_e2m1fn_x4
 RELU = mybir.ActivationFunctionType.Relu
+COPY = mybir.ActivationFunctionType.Copy
 MULT = mybir.AluOpType.mult
 
 P = 128
@@ -21,7 +22,6 @@ HALF = S // 2
 CHUNK = 128
 CHUNKS = S // CHUNK
 W1_SCALAR_M = 56
-VECTOR_CHUNKS = 2
 BANKS = 8
 SCALAR_GROUPS = 12
 
@@ -133,35 +133,45 @@ def tile_picked_echoice_relu_po_kernel(
                 stop=True,
             )
             y_accs[t, cols.start] = y_acc
-        for t, cols in passes:
-            nc.scalar.activation(y[t][:, cols], y_accs[t, cols.start][:], RELU)
 
-        taken = sb.tile([P, SLOTS, V], F32, name="taken")
+        def relu_out(t):
+            for plane, cols in passes:
+                if plane == t:
+                    nc.scalar.activation(y[t][:, cols], y_accs[t, cols.start][:], RELU)
+
+        taken = [sb.tile([P, V], F32, name="taken%d" % t) for t in range(SLOTS)]
         z_bf = [sb.tile([P, CHUNK, SLOTS], BF16, name="z_bf%d" % c, align_bytes=64) for c in range(CHUNKS)]
+        pairs = [sb.tile([P, 2, CHUNK, 2], BF16, name="pairs%d" % c, align_bytes=64) for c in range(CHUNKS)]
 
-        def gather(t):
-            nc.vector.tensor_tensor(taken[:, t, :], y[t][:].indirect(take_sb[:]), wt_sb[:], MULT)
-
-        def z_piece(t, c):
-            return z_bf[c][:, :, t], z[t][:, c * CHUNK : (c + 1) * CHUNK]
-
-        gather(0)
-        for t in range(SLOTS):
+        relu_out(0)
+        nc.vector.tensor_tensor(taken[0][:], y[0][:].indirect(take_sb[:]), wt_sb[:], MULT)
+        relu_out(1)
+        for t in range(1, SLOTS):
             if t + 1 < SLOTS:
-                gather(t + 1)
-            nc.vector.tensor_copy(z[t][:].indirect(take_sb[:]), taken[:, t, :])
+                relu_out(t + 1)
+            nc.scalar.activation(taken[t][:], y[t][:].indirect(take_sb[:]), COPY)
+
+        nc.vector.tensor_copy(z[0][:].indirect(take_sb[:]), taken[0][:])
+        for t in range(1, SLOTS):
+            nc.vector.tensor_tensor(z[t][:].indirect(take_sb[:]), taken[t][:], wt_sb[:], MULT)
+
+        for t in range(SLOTS):
             for c in range(CHUNKS):
-                dst, src = z_piece(t, c)
-                if c >= VECTOR_CHUNKS or t < 2:
-                    nc.scalar.copy(dst, src)
-                elif t == 2:
-                    nc.scalar.copy(z_bf[c][:, :, 2:4], src.unsqueeze(2).to_broadcast([P, CHUNK, 2]))
-                else:
-                    nc.vector.tensor_copy(dst, src)
+                nc.scalar.copy(pairs[c][:, t // 2, :, t % 2], z[t][:, c * CHUNK : (c + 1) * CHUNK])
 
         z_q = sb.tile([P, S], U32, name="z_q", align_bytes=64)
         z_s = sb.tile([P, S], U8, name="z_s", align_bytes=64)
+
+        def weave(c):
+            nc.vector.tensor_copy(
+                z_bf[c][:].rearrange("p n t -> p (n t)").bitcast(I32).rearrange("p (n u) -> p n u", u=2),
+                pairs[c][:].rearrange("p u n e -> p (u n e)").bitcast(I32).rearrange("p (u n) -> p n u", u=2),
+            )
+
+        weave(0)
         for c in range(CHUNKS):
+            if c + 1 < CHUNKS:
+                weave(c + 1)
             chunk = slice(c * CHUNK, (c + 1) * CHUNK)
             nc.vector.quantize_mx(
                 out=z_q[:, chunk].bitcast(FP8X4),

@@ -62,6 +62,8 @@ def tile_picked_echoice_relu_po_kernel(
         nc.sync.dma_start(w1_raw[:, :2, :], w1_rows[:, :2, :])
         nc.sync.dma_start(offs_sb[:], offs)
         xs_table = load_scale_rows_spread(x_scales[0], "xs_table")
+        w2s_raw = load_scale_rows_spread(w2_scales[0], "w2s_raw")
+        nc.sync.dma_start(take_sb[:], take)
         nc.sync.dma_start(w1_raw[:, 2:, :], w1_rows[:, 2:, :])
 
         x_table = sb.tile([P, T], U32, name="x_table", align_bytes=64)
@@ -72,12 +74,19 @@ def tile_picked_echoice_relu_po_kernel(
         x_s = zeroed_scales(S, "x_s")
         move_to_scale_rows(xs_gathered, x_s)
 
-        w2s_raw = load_scale_rows_spread(w2_scales[0], "w2s_raw")
         w2_raw = sb.tile([P, 2 * N], U8, name="w2_raw", align_bytes=64)
         nc.sync.dma_start(w2_raw[:].bitcast(I32), w2_words[0].bitcast(I32))
         wt_sb = sb.tile([P, V], F32, name="wt_sb")
         nc.sync.dma_start(wt_sb[:], wt.rearrange("(p j) v -> p j v", j=SLOTS)[:, 0, :])
-        nc.sync.dma_start(take_sb[:], take)
+
+        w2s_dealt = sb.tile([P, N], U8, name="w2s_dealt", align_bytes=64)
+        nc.vector.tensor_copy(
+            w2s_dealt[:].rearrange("p (t g m) -> p g t m", t=SLOTS, m=16),
+            w2s_raw[:].rearrange("p (g m t) -> p g t m", t=SLOTS, m=16),
+        )
+        w2_s = zeroed_scales(N, "w2_s")
+        move_to_scale_rows(w2s_dealt, w2_s)
+
 
         z = [sb.tile([P, S], F32, name="z%d" % t) for t in range(SLOTS)]
         for t in range(SLOTS):
@@ -99,9 +108,8 @@ def tile_picked_echoice_relu_po_kernel(
         nc.vector.quantize_mx(out=w1_q[:].bitcast(FP8X4), scales=w1_s[:], in_=w1_bf[:])
 
         x_q = sb.tile([P, S], U32, name="x_q", align_bytes=64)
-        for h in range(2):
-            entries = offs_sb[:, h * HALF // GROUP : (h + 1) * HALF // GROUP]
-            nc.vector.tensor_copy(x_q[:, h * HALF : (h + 1) * HALF], x_table[:].indirect(entries))
+        for lo, hi in ((0, HALF), (HALF, HALF + CHUNK), (HALF + CHUNK, S)):
+            nc.vector.tensor_copy(x_q[:, lo:hi], x_table[:].indirect(offs_sb[:, lo // GROUP : hi // GROUP]))
 
         w2_q = sb.tile([P, 2 * N], U8, name="w2_q", align_bytes=64)
         nc.vector.tensor_copy(
@@ -109,19 +117,11 @@ def tile_picked_echoice_relu_po_kernel(
             w2_raw[:].rearrange("p (g m t b) -> p g t m b", t=SLOTS, m=8, b=2),
         )
 
-        w2s_dealt = sb.tile([P, N], U8, name="w2s_dealt", align_bytes=64)
-        nc.vector.tensor_copy(
-            w2s_dealt[:].rearrange("p (t g m) -> p g t m", t=SLOTS, m=16),
-            w2s_raw[:].rearrange("p (g m t) -> p g t m", t=SLOTS, m=16),
-        )
-        w2_s = zeroed_scales(N, "w2_s")
-        move_to_scale_rows(w2s_dealt, w2_s)
-
         y = [sb.tile([P, S], F32, name="y%d" % t) for t in range(SLOTS)]
-        edges = [(0, HALF, HALF + CHUNK, S), (0, HALF, S), (0, S), (0, S)]
+        edges = [(0, HALF, HALF + CHUNK, S), (0, S), (0, S), (0, S)]
         passes = [(t, slice(lo, hi)) for t in range(SLOTS) for lo, hi in zip(edges[t], edges[t][1:])]
         y_accs = {}
-        for bank, (t, cols) in enumerate(sorted(passes, key=lambda item: item[1].stop > HALF)):
+        for bank, (t, cols) in enumerate(passes):
             y_acc = psum.tile([P, cols.stop - cols.start], F32, name="y_acc", tag="bank%d" % bank)
             nc.tensor.matmul_mx(
                 out=y_acc[:],
@@ -141,7 +141,8 @@ def tile_picked_echoice_relu_po_kernel(
 
         taken = [sb.tile([P, V], F32, name="taken%d" % t) for t in range(SLOTS)]
         z_bf = [sb.tile([P, CHUNK, SLOTS], BF16, name="z_bf%d" % c, align_bytes=64) for c in range(CHUNKS)]
-        pairs = [sb.tile([P, 2, CHUNK, 2], BF16, name="pairs%d" % c, align_bytes=64) for c in range(CHUNKS)]
+        pairs = [sb.tile([P, 2, CHUNK, 2], BF16, name="pairs%d" % c, align_bytes=64) for c in range(1, CHUNKS)]
+        pairs = [None] + pairs
 
         relu_out(0)
         nc.vector.tensor_tensor(taken[0][:], y[0][:].indirect(take_sb[:]), wt_sb[:], MULT)
@@ -156,8 +157,15 @@ def tile_picked_echoice_relu_po_kernel(
             nc.vector.tensor_tensor(z[t][:].indirect(take_sb[:]), taken[t][:], wt_sb[:], MULT)
 
         for t in range(SLOTS):
-            for c in range(CHUNKS):
-                nc.scalar.copy(pairs[c][:, t // 2, :, t % 2], z[t][:, c * CHUNK : (c + 1) * CHUNK])
+            nc.scalar.copy(z_bf[0][:, :, t], z[t][:, :CHUNK])
+            for c in range(1, CHUNKS):
+                src = z[t][:, c * CHUNK : (c + 1) * CHUNK]
+                if c == 1 and t == 2:
+                    nc.scalar.copy(pairs[c][:, 1], src.unsqueeze(2).to_broadcast([P, CHUNK, 2]))
+                elif c == 1 and t == 3:
+                    nc.vector.tensor_copy(pairs[c][:, 1, :, 1], src)
+                else:
+                    nc.scalar.copy(pairs[c][:, t // 2, :, t % 2], src)
 
         z_q = sb.tile([P, S], U32, name="z_q", align_bytes=64)
         z_s = sb.tile([P, S], U8, name="z_s", align_bytes=64)
@@ -168,7 +176,6 @@ def tile_picked_echoice_relu_po_kernel(
                 pairs[c][:].rearrange("p u n e -> p (u n e)").bitcast(I32).rearrange("p (u n) -> p n u", u=2),
             )
 
-        weave(0)
         for c in range(CHUNKS):
             if c + 1 < CHUNKS:
                 weave(c + 1)

@@ -141,8 +141,8 @@ def tile_picked_echoice_relu_po_kernel(
 
         taken = [sb.tile([P, V], F32, name="taken%d" % t) for t in range(SLOTS)]
         z_bf = [sb.tile([P, CHUNK, SLOTS], BF16, name="z_bf%d" % c, align_bytes=64) for c in range(CHUNKS)]
-        pairs = [sb.tile([P, 2, CHUNK, 2], BF16, name="pairs%d" % c, align_bytes=64) for c in range(1, CHUNKS)]
-        pairs = [None] + pairs
+        pairs = sb.tile([P, 2, CHUNK, 2], BF16, name="pairs", align_bytes=64)
+        rows = sb.tile([P, SLOTS, HALF], BF16, name="rows", align_bytes=64)
 
         relu_out(0)
         nc.vector.tensor_tensor(taken[0][:], y[0][:].indirect(take_sb[:]), wt_sb[:], MULT)
@@ -157,34 +157,45 @@ def tile_picked_echoice_relu_po_kernel(
             nc.vector.tensor_tensor(z[t][:].indirect(take_sb[:]), taken[t][:], wt_sb[:], MULT)
 
         for t in range(SLOTS):
-            nc.scalar.copy(z_bf[0][:, :, t], z[t][:, :CHUNK])
-            for c in range(1, CHUNKS):
-                src = z[t][:, c * CHUNK : (c + 1) * CHUNK]
-                if c == 1 and t == 2:
-                    nc.scalar.copy(pairs[c][:, 1], src.unsqueeze(2).to_broadcast([P, CHUNK, 2]))
-                elif c == 1 and t == 3:
-                    nc.vector.tensor_copy(pairs[c][:, 1, :, 1], src)
-                else:
-                    nc.scalar.copy(pairs[c][:, t // 2, :, t % 2], src)
+            first, second = z[t][:, :CHUNK], z[t][:, CHUNK:HALF]
+            if t < 2:
+                nc.scalar.copy(z_bf[0][:, :, t], first)
+                nc.scalar.copy(pairs[:, 0, :, t], second)
+            elif t == 2:
+                nc.scalar.copy(z_bf[0][:, :, 2:4], first.unsqueeze(2).to_broadcast([P, CHUNK, 2]))
+                nc.scalar.copy(pairs[:, 1], second.unsqueeze(2).to_broadcast([P, CHUNK, 2]))
+            else:
+                nc.vector.tensor_copy(z_bf[0][:, :, 3], first)
+                nc.vector.tensor_copy(pairs[:, 1, :, 1], second)
+            nc.scalar.copy(rows[:, t, :], z[t][:, HALF:])
 
         z_q = sb.tile([P, S], U32, name="z_q", align_bytes=64)
         z_s = sb.tile([P, S], U8, name="z_s", align_bytes=64)
 
         def weave(c):
             nc.vector.tensor_copy(
-                z_bf[c][:].rearrange("p n t -> p (n t)").bitcast(I32).rearrange("p (n u) -> p n u", u=2),
-                pairs[c][:].rearrange("p u n e -> p (u n e)").bitcast(I32).rearrange("p (u n) -> p n u", u=2),
+                z_bf[c][:].rearrange("p (g n) t -> p g t n", n=4),
+                rows[:, :, c * CHUNK - HALF : (c + 1) * CHUNK - HALF].rearrange("p t (g n) -> p g t n", n=4),
             )
 
-        for c in range(CHUNKS):
-            if c + 1 < CHUNKS:
-                weave(c + 1)
+        def quantise_z(c):
             chunk = slice(c * CHUNK, (c + 1) * CHUNK)
             nc.vector.quantize_mx(
                 out=z_q[:, chunk].bitcast(FP8X4),
                 scales=z_s[:, chunk],
                 in_=z_bf[c][:].rearrange("p n t -> p (n t)"),
             )
+
+        quantise_z(0)
+        nc.vector.tensor_copy(
+            z_bf[1][:].rearrange("p n t -> p (n t)").bitcast(I32).rearrange("p (n u) -> p n u", u=2),
+            pairs[:].rearrange("p u n e -> p (u n e)").bitcast(I32).rearrange("p (u n) -> p n u", u=2),
+        )
+        weave(2)
+        quantise_z(1)
+        weave(3)
+        quantise_z(2)
+        quantise_z(3)
 
         o_q = sb.tile([P, S], U32, name="o_q", align_bytes=64)
         o_s = sb.tile([P, S], U8, name="o_s", align_bytes=64)
@@ -219,7 +230,7 @@ def tile_picked_echoice_relu_po_kernel(
                         start=True,
                         stop=True,
                     )
-                on_vector = (c, planes) in ((0, (2, 3)), (1, (0, 1)))
+                on_vector = (c, planes) == (0, (2, 3))
                 copy_out = nc.vector.tensor_copy if on_vector else nc.scalar.copy
                 held = slice(planes[0], planes[-1] + 1)
                 copy_out(o[:, held, :], o_acc[:])

@@ -21,9 +21,9 @@ K, T, S, V, H, N = 512, 2048, 512, 256, 512, 512
 HALF = S // 2
 CHUNK = 128
 CHUNKS = S // CHUNK
-W1_SCALAR_M = 56
+W1_SCALAR_M = 40
 BANKS = 8
-SCALAR_GROUPS = 12
+SCALAR_GROUPS = 8
 
 FLOPS = 2 * K * H * S + 2 * H * N * S
 

@@ -37,10 +37,10 @@ def tile_picked_echoice_relu_po_kernel(
         sb = ctx.enter_context(tc.tile_pool(name="sb", bufs=1))
         psum = ctx.enter_context(tc.psum_pool(name="psum", bufs=1))
 
-        def load_scale_rows_spread(rows, name):
-            spread = sb.tile([P, rows.shape[1]], U8, name=name, align_bytes=64)
+        def load_scale_rows_spread(source, name):
+            spread = sb.tile([P, source.shape[1]], U8, name=name, align_bytes=64)
             nc.vector.memset(spread[:].bitcast(I32), 0)
-            nc.sync.dma_start(spread[0:P:8, :].bitcast(I32), rows.bitcast(I32))
+            nc.sync.dma_start(spread[0:P:8, :].bitcast(I32), source.bitcast(I32))
             return spread
 
         def zeroed_scales(columns, name):
@@ -87,7 +87,6 @@ def tile_picked_echoice_relu_po_kernel(
         w2_s = zeroed_scales(N, "w2_s")
         move_to_scale_rows(w2s_dealt, w2_s)
 
-
         z = [sb.tile([P, S], F32, name="z%d" % t) for t in range(SLOTS)]
         for t in range(SLOTS):
             nc.vector.memset(z[t][:], 0.0)
@@ -107,8 +106,9 @@ def tile_picked_echoice_relu_po_kernel(
         w1_s = sb.tile([P, H], U8, name="w1_s", align_bytes=64)
         nc.vector.quantize_mx(out=w1_q[:].bitcast(FP8X4), scales=w1_s[:], in_=w1_bf[:])
 
+        pieces = (0, HALF, HALF + CHUNK, S)
         x_q = sb.tile([P, S], U32, name="x_q", align_bytes=64)
-        for lo, hi in ((0, HALF), (HALF, HALF + CHUNK), (HALF + CHUNK, S)):
+        for lo, hi in zip(pieces, pieces[1:]):
             nc.vector.tensor_copy(x_q[:, lo:hi], x_table[:].indirect(offs_sb[:, lo // GROUP : hi // GROUP]))
 
         w2_q = sb.tile([P, 2 * N], U8, name="w2_q", align_bytes=64)
@@ -118,10 +118,10 @@ def tile_picked_echoice_relu_po_kernel(
         )
 
         y = [sb.tile([P, S], F32, name="y%d" % t) for t in range(SLOTS)]
-        edges = [(0, HALF, HALF + CHUNK, S), (0, S), (0, S), (0, S)]
+        edges = [pieces, (0, HALF, S), (0, S), (0, S)]
         passes = [(t, slice(lo, hi)) for t in range(SLOTS) for lo, hi in zip(edges[t], edges[t][1:])]
         y_accs = {}
-        for bank, (t, cols) in enumerate(passes):
+        for bank, (t, cols) in enumerate(sorted(passes, key=lambda item: item[1].stop > HALF)):
             y_acc = psum.tile([P, cols.stop - cols.start], F32, name="y_acc", tag="bank%d" % bank)
             nc.tensor.matmul_mx(
                 out=y_acc[:],
@@ -145,15 +145,17 @@ def tile_picked_echoice_relu_po_kernel(
         rows = sb.tile([P, SLOTS, HALF], BF16, name="rows", align_bytes=64)
 
         relu_out(0)
-        nc.vector.tensor_tensor(taken[0][:], y[0][:].indirect(take_sb[:]), wt_sb[:], MULT)
-        relu_out(1)
+        first_half, second_half = take_sb[:, : V // GROUP // 2], take_sb[:, V // GROUP // 2 :]
+        nc.vector.tensor_copy(taken[0][:, : V // 2], y[0][:].indirect(first_half))
+        nc.scalar.activation(y[1][:, :HALF], y_accs[1, 0][:], RELU)
+        nc.scalar.activation(taken[0][:, V // 2 :], y[0][:].indirect(second_half), COPY)
+        nc.vector.tensor_scalar_max(y[1][:, HALF:], y_accs[1, HALF][:], 0.0)
         for t in range(1, SLOTS):
             if t + 1 < SLOTS:
                 relu_out(t + 1)
             nc.scalar.activation(taken[t][:], y[t][:].indirect(take_sb[:]), COPY)
 
-        nc.vector.tensor_copy(z[0][:].indirect(take_sb[:]), taken[0][:])
-        for t in range(1, SLOTS):
+        for t in range(SLOTS):
             nc.vector.tensor_tensor(z[t][:].indirect(take_sb[:]), taken[t][:], wt_sb[:], MULT)
 
         for t in range(SLOTS):
@@ -172,7 +174,7 @@ def tile_picked_echoice_relu_po_kernel(
         z_q = sb.tile([P, S], U32, name="z_q", align_bytes=64)
         z_s = sb.tile([P, S], U8, name="z_s", align_bytes=64)
 
-        def weave(c):
+        def weave_rows(c):
             nc.vector.tensor_copy(
                 z_bf[c][:].rearrange("p (g n) t -> p g t n", n=4),
                 rows[:, :, c * CHUNK - HALF : (c + 1) * CHUNK - HALF].rearrange("p t (g n) -> p g t n", n=4),
@@ -191,9 +193,9 @@ def tile_picked_echoice_relu_po_kernel(
             z_bf[1][:].rearrange("p n t -> p (n t)").bitcast(I32).rearrange("p (n u) -> p n u", u=2),
             pairs[:].rearrange("p u n e -> p (u n e)").bitcast(I32).rearrange("p (u n) -> p n u", u=2),
         )
-        weave(2)
+        weave_rows(2)
         quantise_z(1)
-        weave(3)
+        weave_rows(3)
         quantise_z(2)
         quantise_z(3)
 

@@ -62,12 +62,13 @@ def tile_picked_echoice_relu_po_kernel(
         nc.sync.dma_start(w1_raw[:, :2, :], w1_rows[:, :2, :])
         nc.sync.dma_start(offs_sb[:], offs)
         xs_table = load_scale_rows_spread(x_scales[0], "xs_table")
-        w2s_raw = load_scale_rows_spread(w2_scales[0], "w2s_raw")
-        nc.sync.dma_start(take_sb[:], take)
         nc.sync.dma_start(w1_raw[:, 2:, :], w1_rows[:, 2:, :])
 
         x_table = sb.tile([P, T], U32, name="x_table", align_bytes=64)
         nc.sync.dma_start(x_table[:].bitcast(I32), x_words[0].rearrange("p n t -> p (n t)").bitcast(I32))
+
+        nc.sync.dma_start(take_sb[:], take)
+        w2s_raw = load_scale_rows_spread(w2_scales[0], "w2s_raw")
 
         xs_gathered = sb.tile([P, S], U8, name="xs_gathered", align_bytes=64)
         nc.vector.tensor_copy(xs_gathered[:], xs_table[:].indirect(offs_sb[:]))
@@ -78,14 +79,6 @@ def tile_picked_echoice_relu_po_kernel(
         nc.sync.dma_start(w2_raw[:].bitcast(I32), w2_words[0].bitcast(I32))
         wt_sb = sb.tile([P, V], F32, name="wt_sb")
         nc.sync.dma_start(wt_sb[:], wt.rearrange("(p j) v -> p j v", j=SLOTS)[:, 0, :])
-
-        w2s_dealt = sb.tile([P, N], U8, name="w2s_dealt", align_bytes=64)
-        nc.vector.tensor_copy(
-            w2s_dealt[:].rearrange("p (t g m) -> p g t m", t=SLOTS, m=16),
-            w2s_raw[:].rearrange("p (g m t) -> p g t m", t=SLOTS, m=16),
-        )
-        w2_s = zeroed_scales(N, "w2_s")
-        move_to_scale_rows(w2s_dealt, w2_s)
 
         z = [sb.tile([P, S], F32, name="z%d" % t) for t in range(SLOTS)]
         for t in range(SLOTS):
@@ -116,6 +109,14 @@ def tile_picked_echoice_relu_po_kernel(
             w2_q[:].rearrange("p (t g m b) -> p g t m b", t=SLOTS, m=8, b=2),
             w2_raw[:].rearrange("p (g m t b) -> p g t m b", t=SLOTS, m=8, b=2),
         )
+
+        w2s_dealt = sb.tile([P, N], U8, name="w2s_dealt", align_bytes=64)
+        nc.vector.tensor_copy(
+            w2s_dealt[:].rearrange("p (t g m) -> p g t m", t=SLOTS, m=16),
+            w2s_raw[:].rearrange("p (g m t) -> p g t m", t=SLOTS, m=16),
+        )
+        w2_s = zeroed_scales(N, "w2_s")
+        move_to_scale_rows(w2s_dealt, w2_s)
 
         y = [sb.tile([P, S], F32, name="y%d" % t) for t in range(SLOTS)]
         edges = [pieces, (0, HALF, S), (0, S), (0, S)]

@@ -106,8 +106,8 @@ def tile_picked_echoice_relu_po_kernel(
 
         w2_q = sb.tile([P, 2 * N], U8, name="w2_q", align_bytes=64)
         nc.vector.tensor_copy(
-            w2_q[:].rearrange("p (t g m b) -> p g t m b", t=SLOTS, m=8, b=2),
-            w2_raw[:].rearrange("p (g m t b) -> p g t m b", t=SLOTS, m=8, b=2),
+            w2_q[:].bitcast(U16).rearrange("p (t g m) -> p g t m", t=SLOTS, m=8),
+            w2_raw[:].bitcast(U16).rearrange("p (g m t) -> p g t m", t=SLOTS, m=8),
         )
 
         w2s_dealt = sb.tile([P, N], U8, name="w2s_dealt", align_bytes=64)
@@ -150,7 +150,7 @@ def tile_picked_echoice_relu_po_kernel(
         nc.vector.tensor_copy(taken[0][:, : V // 2], y[0][:].indirect(first_half))
         nc.scalar.activation(y[1][:, :HALF], y_accs[1, 0][:], RELU)
         nc.scalar.activation(taken[0][:, V // 2 :], y[0][:].indirect(second_half), COPY)
-        nc.vector.tensor_scalar_max(y[1][:, HALF:], y_accs[1, HALF][:], 0.0)
+        nc.scalar.activation(y[1][:, HALF:], y_accs[1, HALF][:], RELU)
         for t in range(1, SLOTS):
             if t + 1 < SLOTS:
                 relu_out(t + 1)

@@ -237,9 +237,9 @@ def tile_picked_echoice_relu_po_kernel(
                 copy_out = nc.vector.tensor_copy if on_vector else nc.scalar.copy
                 held = slice(planes[0], planes[-1] + 1)
                 copy_out(o[:, held, :], o_acc[:])
-                if cols.stop <= HALF:
+                if not last:
                     nc.sync.dma_start(out_planes[:, held, cols], o[:, held, :])
-            if cols.stop > HALF:
+            if last:
                 nc.sync.dma_start(out_planes[:, :, cols], o[:])
 
             o_bf = sb.tile([P, CHUNK * SLOTS], BF16, name="o_bf%d" % c, align_bytes=64)
@@ -258,5 +258,4 @@ def tile_picked_echoice_relu_po_kernel(
             quantise_out(c)
 
         for q in range(4):
-            queue = nc.sync if q % 2 == 0 else nc.scalar
-            queue.dma_start(out_2[0, 4 * q : 4 * q + 4, :].bitcast(I32), o_s[32 * q : 32 * q + 4, :].bitcast(I32))
+            nc.sync.dma_start(out_2[0, 4 * q : 4 * q + 4, :].bitcast(I32), o_s[32 * q : 32 * q + 4, :].bitcast(I32))

@@ -175,8 +175,8 @@ def tile_picked_echoice_relu_po_kernel(
         z_q = sb.tile([P, S], U32, name="z_q", align_bytes=64)
         z_s = sb.tile([P, S], U8, name="z_s", align_bytes=64)
 
-        def weave_rows(c):
-            nc.vector.tensor_copy(
+        def weave_rows(c, copy):
+            copy(
                 z_bf[c][:].rearrange("p (g n) t -> p g t n", n=4),
                 rows[:, :, c * CHUNK - HALF : (c + 1) * CHUNK - HALF].rearrange("p t (g n) -> p g t n", n=4),
             )
@@ -194,9 +194,9 @@ def tile_picked_echoice_relu_po_kernel(
             z_bf[1][:].rearrange("p n t -> p (n t)").bitcast(I32).rearrange("p (n u) -> p n u", u=2),
             pairs[:].rearrange("p u n e -> p (u n e)").bitcast(I32).rearrange("p (u n) -> p n u", u=2),
         )
-        weave_rows(2)
+        weave_rows(2, nc.vector.tensor_copy)
         quantise_z(1)
-        weave_rows(3)
+        weave_rows(3, nc.scalar.copy)
         quantise_z(2)
         quantise_z(3)
 
@@ -233,10 +233,8 @@ def tile_picked_echoice_relu_po_kernel(
                         start=True,
                         stop=True,
                     )
-                on_vector = (c, planes) == (0, (2, 3))
-                copy_out = nc.vector.tensor_copy if on_vector else nc.scalar.copy
                 held = slice(planes[0], planes[-1] + 1)
-                copy_out(o[:, held, :], o_acc[:])
+                nc.scalar.copy(o[:, held, :], o_acc[:])
                 if not last:
                     nc.sync.dma_start(out_planes[:, held, cols], o[:, held, :])
             if last:

@@ -142,7 +142,7 @@ def tile_picked_echoice_relu_po_kernel(
 
         taken = [sb.tile([P, V], F32, name="taken%d" % t) for t in range(SLOTS)]
         z_bf = [sb.tile([P, CHUNK, SLOTS], BF16, name="z_bf%d" % c, align_bytes=64) for c in range(CHUNKS)]
-        pairs = sb.tile([P, 2, CHUNK, 2], BF16, name="pairs", align_bytes=64)
+        pairs = sb.tile([P, 2, HALF, 2], BF16, name="pairs", align_bytes=64)
         rows = sb.tile([P, SLOTS, HALF], BF16, name="rows", align_bytes=64)
 
         relu_out(0)
@@ -159,27 +159,34 @@ def tile_picked_echoice_relu_po_kernel(
         for t in range(SLOTS):
             nc.vector.tensor_tensor(z[t][:].indirect(take_sb[:]), taken[t][:], wt_sb[:], MULT)
 
-        for t in range(SLOTS):
-            first, second = z[t][:, :CHUNK], z[t][:, CHUNK:HALF]
-            if t < 2:
-                nc.scalar.copy(z_bf[0][:, :, t], first)
-                nc.scalar.copy(pairs[:, 0, :, t], second)
-            elif t == 2:
-                nc.scalar.copy(z_bf[0][:, :, 2:4], first.unsqueeze(2).to_broadcast([P, CHUNK, 2]))
-                nc.scalar.copy(pairs[:, 1], second.unsqueeze(2).to_broadcast([P, CHUNK, 2]))
-            else:
-                nc.vector.tensor_copy(z_bf[0][:, :, 3], first)
-                nc.vector.tensor_copy(pairs[:, 1, :, 1], second)
-            nc.scalar.copy(rows[:, t, :], z[t][:, HALF:])
-
-        z_q = sb.tile([P, S], U32, name="z_q", align_bytes=64)
-        z_s = sb.tile([P, S], U8, name="z_s", align_bytes=64)
+        def weave_pairs(c, copy):
+            words = pairs[:].rearrange("p u n e -> p (u n e)").bitcast(U32).rearrange("p (u n) -> p n u", u=2)
+            copy(
+                z_bf[c][:].rearrange("p n t -> p (n t)").bitcast(U32).rearrange("p (n u) -> p n u", u=2),
+                words[:, c * CHUNK : (c + 1) * CHUNK, :],
+            )
 
         def weave_rows(c, copy):
             copy(
                 z_bf[c][:].rearrange("p (g n) t -> p g t n", n=4),
                 rows[:, :, c * CHUNK - HALF : (c + 1) * CHUNK - HALF].rearrange("p t (g n) -> p g t n", n=4),
             )
+
+        for t in range(SLOTS):
+            if t < 2:
+                nc.scalar.copy(pairs[:, 0, :, t], z[t][:, :HALF])
+            elif t == 2:
+                for c in range(2):
+                    chunk = slice(c * CHUNK, (c + 1) * CHUNK)
+                    nc.scalar.copy(pairs[:, 1, chunk], z[t][:, chunk].unsqueeze(2).to_broadcast([P, CHUNK, 2]))
+                weave_pairs(0, nc.scalar.copy)
+            else:
+                nc.vector.tensor_copy(z_bf[0][:, :, 3], z[t][:, :CHUNK])
+                nc.vector.tensor_copy(pairs[:, 1, CHUNK:, 1], z[t][:, CHUNK:HALF])
+            nc.scalar.copy(rows[:, t, :], z[t][:, HALF:])
+
+        z_q = sb.tile([P, S], U32, name="z_q", align_bytes=64)
+        z_s = sb.tile([P, S], U8, name="z_s", align_bytes=64)
 
         def quantise_z(c):
             chunk = slice(c * CHUNK, (c + 1) * CHUNK)
@@ -190,10 +197,7 @@ def tile_picked_echoice_relu_po_kernel(
             )
 
         quantise_z(0)
-        nc.vector.tensor_copy(
-            z_bf[1][:].rearrange("p n t -> p (n t)").bitcast(I32).rearrange("p (n u) -> p n u", u=2),
-            pairs[:].rearrange("p u n e -> p (u n e)").bitcast(I32).rearrange("p (u n) -> p n u", u=2),
-        )
+        weave_pairs(1, nc.vector.tensor_copy)
         weave_rows(2, nc.vector.tensor_copy)
         quantise_z(1)
         weave_rows(3, nc.scalar.copy)

@@ -215,9 +215,9 @@ def tile_picked_echoice_relu_po_kernel(
         def quantise_out(c):
             cols, o_bf = rounded[c]
             nc.vector.quantize_mx(out=o_q[:, cols].bitcast(FP8X4), scales=o_s[:, cols], in_=o_bf[:])
-            if c % 2 == 1:
-                half = slice(cols.stop - HALF, cols.stop)
-                nc.sync.dma_start(out_words[:, half], o_q[:, half].bitcast(I32))
+
+        def store_codes(half):
+            nc.sync.dma_start(out_words[:, half], o_q[:, half].bitcast(I32))
 
         for c in range(CHUNKS):
             cols = slice(c * CHUNK, (c + 1) * CHUNK)
@@ -241,6 +241,8 @@ def tile_picked_echoice_relu_po_kernel(
                 nc.scalar.copy(o[:, held, :], o_acc[:])
                 if not last:
                     nc.sync.dma_start(out_planes[:, held, cols], o[:, held, :])
+            if c == CHUNKS - 2:
+                store_codes(slice(0, HALF))
             if last:
                 nc.sync.dma_start(out_planes[:, :, cols], o[:])
 
@@ -253,11 +255,13 @@ def tile_picked_echoice_relu_po_kernel(
             else:
                 nc.vector.tensor_copy(bf_dst, bf_src)
             rounded.append((cols, o_bf))
-            if 0 < c < CHUNKS - 1:
-                quantise_out(c - 1)
+            if c < CHUNKS - 2:
+                quantise_out(c)
         for c, share in zip(range(CHUNKS - 2, CHUNKS), scalar_shares):
             nc.scalar.copy(*share)
             quantise_out(c)
+
+        store_codes(slice(HALF, S))
 
         for q in range(4):
             nc.sync.dma_start(out_2[0, 4 * q : 4 * q + 4, :].bitcast(I32), o_s[32 * q : 32 * q + 4, :].bitcast(I32))

@@ -181,8 +181,9 @@ def tile_picked_echoice_relu_po_kernel(
                     nc.scalar.copy(pairs[:, 1, chunk], z[t][:, chunk].unsqueeze(2).to_broadcast([P, CHUNK, 2]))
                 weave_pairs(0, nc.scalar.copy)
             else:
-                nc.vector.tensor_copy(z_bf[0][:, :, 3], z[t][:, :CHUNK])
-                nc.vector.tensor_copy(pairs[:, 1, CHUNK:, 1], z[t][:, CHUNK:HALF])
+                weave_pairs(1, nc.vector.tensor_copy)
+                for c in range(2):
+                    nc.vector.tensor_copy(z_bf[c][:, :, 3], z[t][:, c * CHUNK : (c + 1) * CHUNK])
             nc.scalar.copy(rows[:, t, :], z[t][:, HALF:])
 
         z_q = sb.tile([P, S], U32, name="z_q", align_bytes=64)
@@ -197,7 +198,6 @@ def tile_picked_echoice_relu_po_kernel(
             )
 
         quantise_z(0)
-        weave_pairs(1, nc.vector.tensor_copy)
         weave_rows(2, nc.vector.tensor_copy)
         quantise_z(1)
         weave_rows(3, nc.scalar.copy)

@@ -184,7 +184,11 @@ def tile_picked_echoice_relu_po_kernel(
                 weave_pairs(1, nc.vector.tensor_copy)
                 for c in range(2):
                     nc.vector.tensor_copy(z_bf[c][:, :, 3], z[t][:, c * CHUNK : (c + 1) * CHUNK])
-            nc.scalar.copy(rows[:, t, :], z[t][:, HALF:])
+            if t < 3:
+                nc.scalar.copy(rows[:, t, :], z[t][:, HALF:])
+            else:
+                nc.scalar.copy(rows[:, t, CHUNK:], z[t][:, HALF + CHUNK :])
+                nc.scalar.copy(rows[:, t, :CHUNK], z[t][:, HALF : HALF + CHUNK])
 
         z_q = sb.tile([P, S], U32, name="z_q", align_bytes=64)
         z_s = sb.tile([P, S], U8, name="z_s", align_bytes=64)

@@ -43,9 +43,12 @@ def tile_picked_echoice_relu_po_kernel(
             nc.sync.dma_start(spread[0:P:8, :].bitcast(I32), source.bitcast(I32))
             return spread
 
-        def zeroed_scales(columns, name):
-            scales = sb.tile([P, columns], U8, name=name, align_bytes=64)
-            nc.vector.memset(scales[:].bitcast(I32), 0)
+        def placed(width, place, name):
+            tile = sb.tile([P, 64 * place + width], U8, name=name, align_bytes=256)
+            return tile[:, 64 * place :]
+
+        def zeroed(scales):
+            nc.vector.memset(scales.bitcast(I32), 0)
             return scales
 
         def move_to_scale_rows(spread, scales):
@@ -72,7 +75,7 @@ def tile_picked_echoice_relu_po_kernel(
 
         xs_gathered = sb.tile([P, S], U8, name="xs_gathered", align_bytes=64)
         nc.vector.tensor_copy(xs_gathered[:], xs_table[:].indirect(offs_sb[:]))
-        x_s = zeroed_scales(S, "x_s")
+        x_s = zeroed(sb.tile([P, S], U8, name="x_s", align_bytes=64)[:])
         move_to_scale_rows(xs_gathered, x_s)
 
         w2_raw = sb.tile([P, 2 * N], U8, name="w2_raw", align_bytes=64)
@@ -104,9 +107,9 @@ def tile_picked_echoice_relu_po_kernel(
         for lo, hi in zip(pieces, pieces[1:]):
             nc.vector.tensor_copy(x_q[:, lo:hi], x_table[:].indirect(offs_sb[:, lo // GROUP : hi // GROUP]))
 
-        w2_q = sb.tile([P, 2 * N], U8, name="w2_q", align_bytes=64)
+        w2_q = placed(2 * N, 0, "w2_q")
         nc.vector.tensor_copy(
-            w2_q[:].bitcast(U16).rearrange("p (t g m) -> p g t m", t=SLOTS, m=8),
+            w2_q.bitcast(U16).rearrange("p (t g m) -> p g t m", t=SLOTS, m=8),
             w2_raw[:].bitcast(U16).rearrange("p (g m t) -> p g t m", t=SLOTS, m=8),
         )
 
@@ -115,7 +118,7 @@ def tile_picked_echoice_relu_po_kernel(
             w2s_dealt[:].rearrange("p (t g m) -> p g t m", t=SLOTS, m=16),
             w2s_raw[:].rearrange("p (g m t) -> p g t m", t=SLOTS, m=16),
         )
-        w2_s = zeroed_scales(N, "w2_s")
+        w2_s = zeroed(placed(N, 1, "w2_s"))
         move_to_scale_rows(w2s_dealt, w2_s)
 
         y = [sb.tile([P, S], F32, name="y%d" % t) for t in range(SLOTS)]
@@ -190,8 +193,8 @@ def tile_picked_echoice_relu_po_kernel(
                 nc.scalar.copy(rows[:, t, CHUNK:], z[t][:, HALF + CHUNK :])
                 nc.scalar.copy(rows[:, t, :CHUNK], z[t][:, HALF : HALF + CHUNK])
 
-        z_q = sb.tile([P, S], U32, name="z_q", align_bytes=64)
-        z_s = sb.tile([P, S], U8, name="z_s", align_bytes=64)
+        z_q = placed(4 * S, 2, "z_q").bitcast(U32)
+        z_s = placed(S, 3, "z_s")
 
         def quantise_z(c):
             chunk = slice(c * CHUNK, (c + 1) * CHUNK)

from contextlib import ExitStack

import concourse.mybir as mybir

F32 = mybir.dt.float32
BF16 = mybir.dt.bfloat16
I32 = mybir.dt.int32
U32 = mybir.dt.uint32
U16 = mybir.dt.uint16
U8 = mybir.dt.uint8
FP8X4 = mybir.dt.float8_e4m3fn_x4
FP4X4 = mybir.dt.float4_e2m1fn_x4
RELU = mybir.ActivationFunctionType.Relu
COPY = mybir.ActivationFunctionType.Copy
MULT = mybir.AluOpType.mult

P = 128
SLOTS = 4
GROUP = 16
K, T, S, V, H, N = 512, 2048, 512, 256, 512, 512
HALF = S // 2
CHUNK = 128
CHUNKS = S // CHUNK
W1_SCALAR_M = 40
BANKS = 8
SCALAR_GROUPS = 8

FLOPS = 2 * K * H * S + 2 * H * N * S


def tile_picked_echoice_relu_po_kernel(
    tc, x_words, x_scales, w1, wt, w2_words, w2_scales, offs, take, out_0, out_1, out_2
):
    nc = tc.nc
    with ExitStack() as ctx:
        lists = ctx.enter_context(tc.tile_pool(name="lists", bufs=1))
        sb = ctx.enter_context(tc.tile_pool(name="sb", bufs=1))
        psum = ctx.enter_context(tc.psum_pool(name="psum", bufs=1))

        def load_scale_rows_spread(source, name):
            spread = sb.tile([P, source.shape[1]], U8, name=name, align_bytes=64)
            nc.vector.memset(spread[:].bitcast(I32), 0)
            nc.sync.dma_start(spread[0:P:8, :].bitcast(I32), source.bitcast(I32))
            return spread

        def placed(width, place, name):
            tile = sb.tile([P, 64 * place + width], U8, name=name, align_bytes=256)
            return tile[:, 64 * place :]

        def zeroed(scales):
            nc.vector.memset(scales.bitcast(I32), 0)
            return scales

        def move_to_scale_rows(spread, scales):
            for q in range(4):
                nc.sync.dma_start(
                    scales[32 * q : 32 * q + 4, :].bitcast(I32), spread[32 * q : 32 * q + 32 : 8, :].bitcast(I32)
                )

        offs_sb = lists.tile([P, S // GROUP], U16, name="offs_sb")
        take_sb = lists.tile([P, V // GROUP], U16, name="take_sb")

        w1_rows = w1.rearrange("(p j) c -> p j c", j=SLOTS)
        w1_raw = sb.tile([P, SLOTS, H], F32, name="w1_raw")
        nc.sync.dma_start(w1_raw[:, :2, :], w1_rows[:, :2, :])
        nc.sync.dma_start(offs_sb[:], offs)
        xs_table = load_scale_rows_spread(x_scales[0], "xs_table")
        nc.sync.dma_start(w1_raw[:, 2:, :], w1_rows[:, 2:, :])

        x_table = sb.tile([P, T], U32, name="x_table", align_bytes=64)
        nc.sync.dma_start(x_table[:].bitcast(I32), x_words[0].rearrange("p n t -> p (n t)").bitcast(I32))

        nc.sync.dma_start(take_sb[:], take)
        w2s_raw = load_scale_rows_spread(w2_scales[0], "w2s_raw")

        xs_gathered = sb.tile([P, S], U8, name="xs_gathered", align_bytes=64)
        nc.vector.tensor_copy(xs_gathered[:], xs_table[:].indirect(offs_sb[:]))
        x_s = zeroed(sb.tile([P, S], U8, name="x_s", align_bytes=64)[:])
        move_to_scale_rows(xs_gathered, x_s)

        w2_raw = sb.tile([P, 2 * N], U8, name="w2_raw", align_bytes=64)
        nc.sync.dma_start(w2_raw[:].bitcast(I32), w2_words[0].bitcast(I32))
        wt_sb = sb.tile([P, V], F32, name="wt_sb")
        nc.sync.dma_start(wt_sb[:], wt.rearrange("(p j) v -> p j v", j=SLOTS)[:, 0, :])

        z = [sb.tile([P, S], F32, name="z%d" % t) for t in range(SLOTS)]
        for t in range(SLOTS):
            nc.vector.memset(z[t][:], 0.0)

        w1_bf = sb.tile([P, SLOTS * H], BF16, name="w1_bf", align_bytes=64)
        for j in (0, 2):
            nc.scalar.copy(
                w1_bf[:].rearrange("p (t m j) -> p t m j", t=SLOTS, j=SLOTS)[:, :, :W1_SCALAR_M, j : j + 2],
                w1_raw[:, j : j + 2, :].rearrange("p j (m t) -> p t m j", t=SLOTS)[:, :, :W1_SCALAR_M, :],
            )
        nc.vector.tensor_copy(
            w1_bf[:].rearrange("p (t m j) -> p m t j", t=SLOTS, j=SLOTS)[:, W1_SCALAR_M:],
            w1_raw[:].rearrange("p j (m t) -> p m t j", t=SLOTS)[:, W1_SCALAR_M:],
        )

        w1_q = sb.tile([P, H], U32, name="w1_q", align_bytes=64)
        w1_s = sb.tile([P, H], U8, name="w1_s", align_bytes=64)
        nc.vector.quantize_mx(out=w1_q[:].bitcast(FP8X4), scales=w1_s[:], in_=w1_bf[:])

        pieces = (0, HALF, HALF + CHUNK, S)
        x_q = sb.tile([P, S], U32, name="x_q", align_bytes=64)
        for lo, hi in zip(pieces, pieces[1:]):
            nc.vector.tensor_copy(x_q[:, lo:hi], x_table[:].indirect(offs_sb[:, lo // GROUP : hi // GROUP]))

        w2_q = placed(2 * N, 0, "w2_q")
        nc.vector.tensor_copy(
            w2_q.bitcast(U16).rearrange("p (t g m) -> p g t m", t=SLOTS, m=8),
            w2_raw[:].bitcast(U16).rearrange("p (g m t) -> p g t m", t=SLOTS, m=8),
        )

        w2s_dealt = sb.tile([P, N], U8, name="w2s_dealt", align_bytes=64)
        nc.vector.tensor_copy(
            w2s_dealt[:].rearrange("p (t g m) -> p g t m", t=SLOTS, m=16),
            w2s_raw[:].rearrange("p (g m t) -> p g t m", t=SLOTS, m=16),
        )
        w2_s = zeroed(placed(N, 1, "w2_s"))
        move_to_scale_rows(w2s_dealt, w2_s)

        y = [sb.tile([P, S], F32, name="y%d" % t) for t in range(SLOTS)]
        edges = [pieces, (0, HALF, S), (0, S), (0, S)]
        passes = [(t, slice(lo, hi)) for t in range(SLOTS) for lo, hi in zip(edges[t], edges[t][1:])]
        y_accs = {}
        for bank, (t, cols) in enumerate(sorted(passes, key=lambda item: item[1].stop > HALF)):
            y_acc = psum.tile([P, cols.stop - cols.start], F32, name="y_acc", tag="bank%d" % bank)
            nc.tensor.matmul_mx(
                out=y_acc[:],
                lhsT=w1_q[:, t * P : (t + 1) * P].bitcast(FP8X4),
                lhsT_scale=w1_s[:, t * P : (t + 1) * P],
                rhs=x_q[:, cols].bitcast(FP8X4),
                rhs_scale=x_s[:, cols],
                start=True,
                stop=True,
            )
            y_accs[t, cols.start] = y_acc

        def relu_out(t):
            for plane, cols in passes:
                if plane == t:
                    nc.scalar.activation(y[t][:, cols], y_accs[t, cols.start][:], RELU)

        taken = [sb.tile([P, V], F32, name="taken%d" % t) for t in range(SLOTS)]
        z_bf = [sb.tile([P, CHUNK, SLOTS], BF16, name="z_bf%d" % c, align_bytes=64) for c in range(CHUNKS)]
        pairs = sb.tile([P, 2, HALF, 2], BF16, name="pairs", align_bytes=64)
        rows = sb.tile([P, SLOTS, HALF], BF16, name="rows", align_bytes=64)

        relu_out(0)
        first_half, second_half = take_sb[:, : V // GROUP // 2], take_sb[:, V // GROUP // 2 :]
        nc.vector.tensor_copy(taken[0][:, : V // 2], y[0][:].indirect(first_half))
        nc.scalar.activation(y[1][:, :HALF], y_accs[1, 0][:], RELU)
        nc.scalar.activation(taken[0][:, V // 2 :], y[0][:].indirect(second_half), COPY)
        nc.scalar.activation(y[1][:, HALF:], y_accs[1, HALF][:], RELU)
        for t in range(1, SLOTS):
            if t + 1 < SLOTS:
                relu_out(t + 1)
            nc.scalar.activation(taken[t][:], y[t][:].indirect(take_sb[:]), COPY)

        for t in range(SLOTS):
            nc.vector.tensor_tensor(z[t][:].indirect(take_sb[:]), taken[t][:], wt_sb[:], MULT)

        def weave_pairs(c, copy):
            words = pairs[:].rearrange("p u n e -> p (u n e)").bitcast(U32).rearrange("p (u n) -> p n u", u=2)
            copy(
                z_bf[c][:].rearrange("p n t -> p (n t)").bitcast(U32).rearrange("p (n u) -> p n u", u=2),
                words[:, c * CHUNK : (c + 1) * CHUNK, :],
            )

        def weave_rows(c, copy):
            copy(
                z_bf[c][:].rearrange("p (g n) t -> p g t n", n=4),
                rows[:, :, c * CHUNK - HALF : (c + 1) * CHUNK - HALF].rearrange("p t (g n) -> p g t n", n=4),
            )

        for t in range(SLOTS):
            if t < 2:
                nc.scalar.copy(pairs[:, 0, :, t], z[t][:, :HALF])
            elif t == 2:
                for c in range(2):
                    chunk = slice(c * CHUNK, (c + 1) * CHUNK)
                    nc.scalar.copy(pairs[:, 1, chunk], z[t][:, chunk].unsqueeze(2).to_broadcast([P, CHUNK, 2]))
                weave_pairs(0, nc.scalar.copy)
            else:
                weave_pairs(1, nc.vector.tensor_copy)
                for c in range(2):
                    nc.vector.tensor_copy(z_bf[c][:, :, 3], z[t][:, c * CHUNK : (c + 1) * CHUNK])
            if t < 3:
                nc.scalar.copy(rows[:, t, :], z[t][:, HALF:])
            else:
                nc.scalar.copy(rows[:, t, CHUNK:], z[t][:, HALF + CHUNK :])
                nc.scalar.copy(rows[:, t, :CHUNK], z[t][:, HALF : HALF + CHUNK])

        z_q = placed(4 * S, 2, "z_q").bitcast(U32)
        z_s = placed(S, 3, "z_s")

        def quantise_z(c):
            chunk = slice(c * CHUNK, (c + 1) * CHUNK)
            nc.vector.quantize_mx(
                out=z_q[:, chunk].bitcast(FP8X4),
                scales=z_s[:, chunk],
                in_=z_bf[c][:].rearrange("p n t -> p (n t)"),
            )

        quantise_z(0)
        weave_rows(2, nc.vector.tensor_copy)
        quantise_z(1)
        weave_rows(3, nc.scalar.copy)
        quantise_z(2)
        quantise_z(3)

        o_q = sb.tile([P, S], U32, name="o_q", align_bytes=64)
        o_s = sb.tile([P, S], U8, name="o_s", align_bytes=64)
        out_planes = out_0.rearrange("(p t) c -> p t c", t=SLOTS)
        out_words = out_1[0].rearrange("p n t -> p (n t)").bitcast(I32)
        banks_used = 0
        rounded = []
        scalar_shares = []

        def quantise_out(c):
            cols, o_bf = rounded[c]
            nc.vector.quantize_mx(out=o_q[:, cols].bitcast(FP8X4), scales=o_s[:, cols], in_=o_bf[:])

        def store_codes(half):
            nc.sync.dma_start(out_words[:, half], o_q[:, half].bitcast(I32))

        for c in range(CHUNKS):
            cols = slice(c * CHUNK, (c + 1) * CHUNK)
            last = c == CHUNKS - 1
            o = sb.tile([P, SLOTS, CHUNK], F32, name="o%d" % c)
            by_bank = [(0,), (1,), (2, 3)] if c == 0 else [(0, 1), (2,), (3,)] if last else [(0, 1), (2, 3)]
            for planes in by_bank:
                o_acc = psum.tile([P, len(planes), CHUNK], F32, name="o_acc", tag="bank%d" % (banks_used % BANKS))
                banks_used = banks_used + 1
                for place, t in enumerate(planes):
                    nc.tensor.matmul_mx(
                        out=o_acc[:, place, :],
                        lhsT=w2_q[:, 2 * t * P : 2 * (t + 1) * P].bitcast(FP4X4),
                        lhsT_scale=w2_s[:, t * P : (t + 1) * P],
                        rhs=z_q[:, cols].bitcast(FP8X4),
                        rhs_scale=z_s[:, cols],
                        start=True,
                        stop=True,
                    )
                held = slice(planes[0], planes[-1] + 1)
                nc.scalar.copy(o[:, held, :], o_acc[:])
                if not last:
                    nc.sync.dma_start(out_planes[:, held, cols], o[:, held, :])
            if c == CHUNKS - 2:
                store_codes(slice(0, HALF))
            if last:
                nc.sync.dma_start(out_planes[:, :, cols], o[:])

            o_bf = sb.tile([P, CHUNK * SLOTS], BF16, name="o_bf%d" % c, align_bytes=64)
            bf_dst = o_bf[:].rearrange("p (g n t) -> p g t n", n=4, t=SLOTS)
            bf_src = o[:].rearrange("p t (g n) -> p g t n", n=4)
            if c >= CHUNKS - 2:
                nc.vector.tensor_copy(bf_dst[:, SCALAR_GROUPS:], bf_src[:, SCALAR_GROUPS:])
                scalar_shares.append((bf_dst[:, :SCALAR_GROUPS], bf_src[:, :SCALAR_GROUPS]))
            else:
                nc.vector.tensor_copy(bf_dst, bf_src)
            rounded.append((cols, o_bf))
            if c < CHUNKS - 2:
                quantise_out(c)
        for c, share in zip(range(CHUNKS - 2, CHUNKS), scalar_shares):
            nc.scalar.copy(*share)
            quantise_out(c)

        store_codes(slice(HALF, S))

        for q in range(4):
            nc.sync.dma_start(out_2[0, 4 * q : 4 * q + 4, :].bitcast(I32), o_s[32 * q : 32 * q + 4, :].bitcast(I32))
